import numpy as np, ml_dtypes
CORES = [3,11,19,27,35,43,51,59]
N = 8
import mx_ref
BF = ml_dtypes.bfloat16
def gcols(t, e):
    v = np.concatenate([t.reshape(8, 16, -1, 4), np.zeros((8, 16, 1, 4), BF)], axis=2)
    return np.ascontiguousarray(np.stack([v[g][:, e[g]] for g in range(8)])).reshape(128, -1)
def tile(rs):
    return np.stack(rs, axis=2).reshape(128, -1).astype(BF)
def pick(q, e):
    c = np.concatenate([q[0].reshape(128, -1, 4), np.zeros((128, 1, 4), np.uint8)], axis=1); s = np.concatenate([q[1], np.ones((16, 1), np.uint8)], axis=1)
    return (np.ascontiguousarray(c[:, e].reshape(128, -1)), np.ascontiguousarray(s[:, e]))
def join(*qs):
    return (np.concatenate([q[0] for q in qs], axis=1), np.concatenate([q[1] for q in qs], axis=1))
def put(q, e, v):
    c, s = q[0].reshape(128, -1, 4).copy(), q[1].copy(); c[:, e] = v[0].reshape(128, -1, 4); s[:, e] = v[1]
    return (c.reshape(128, -1), s)
def pk(c, s):
    return (np.ascontiguousarray(c), mx_ref.live(s))
def emit(q):
    return q[0], q[1]
def packed(v, rng):
    q = [mx_ref.quantize(np.ascontiguousarray(v[r])) for r in range(N)]
    return np.stack([a for a, b in q]), np.stack([mx_ref.plane(b, rng) for a, b in q])
def values_of_codes():
    e, c = np.zeros((128, 128, 4), np.float32), np.zeros((128, 2, 4), np.uint8)
    e[np.arange(128), np.arange(128), 0] = 1
    c[:127, :, 0] = np.arange(256).reshape(2, 128).T[:127]
    return mx_ref.matmul(mx_ref.quantize(e.reshape(128, 512).astype(BF)), (c.reshape(128, 8), np.full((16, 2), 127, np.uint8))).T.reshape(-1).astype(np.float64)
CODE_VALUE, SCALE_VALUE = values_of_codes(), 2.0 ** (np.arange(256) - 127.0)
def decode(q):
    return (CODE_VALUE[q[0]].reshape(16, 8, -1, 4) * SCALE_VALUE[q[1]][:, None, :, None] + 0.0).reshape(128, -1).astype(np.float32)
def f(rng, *shape):
    return mx_ref.flush((rng.standard_normal(shape, dtype=np.float32) * np.exp2(rng.integers(-2, 3, shape[:-1] + (1,)))).astype(BF))
def wide(rng, *shape, cols=0):
    v = rng.standard_normal(shape, dtype=np.float32) * np.exp2(rng.integers(-12, 13, shape)).astype(np.float32)
    if cols: v *= np.repeat(np.exp2(rng.integers(-cols, cols + 1, shape[:-2] + (1, shape[-1] // 4))) * (rng.random(shape[:-2] + (1, shape[-1] // 4)) > 0.0625), 4, axis=-1).astype(np.float32)
    return mx_ref.flush(v.astype(BF))
T, M, R, L = 448, 128, 3, 3
def clock(z):
    step = 1 + np.sum(z.reshape(8, 16, T) > 0, axis=1)
    c = np.cumsum(step, axis=1)
    s = c[:, -1:]
    first = np.argmax(M * c[:, None, :] > np.arange(M)[:, None] * s[:, :, None], axis=2)
    phase = M * (c - step) // s
    return c, first, phase
def big(v, k):
    v = v.astype(np.float32) * np.float32(k)
    v[np.abs(v) < np.float32(2.0 ** -16)] = 0
    return v.astype(BF)
def dense(rng):
    return np.array(f(rng, N, 128, 2048))
def weights(rng, w):
    c, p = packed(w, rng)
    return {"wc": c, "ws": p}
def setup_inputs(rng):
    return {"x": big(f(rng, N, 128, 4 * T), 1), "u": np.array(f(rng, N, 128, 512)), **weights(rng, dense(rng))}
def signals(rng, c):
    p = np.arange(128)
    x = big(f(rng, N, 128, 4 * T), 1).reshape(N, 128, T, 4)
    order = np.argsort(rng.random((8, 16)), axis=1)
    up = (order[:, :, None] < c[:, :, None] - 1).reshape(N, 128, T)
    size = (1 + rng.random((N, 128, T))) * 2.0 ** rng.integers(0, 2, (N, 128, T))
    x[..., 0] = (np.where(up, size, -size * (rng.random((N, 128, T)) > 0.25)) + 0.0).astype(np.float32).astype(BF)
    u = np.zeros((N, 128, 128, 4), BF)
    u[:, p, p, 0] = (2.0 ** rng.integers(-3, 4, (N, 128))).astype(np.float32).astype(BF)
    w = dense(rng).reshape(N, 128, 4, 128, 4)
    w[:, :, 0] = 0
    w[:, p, 0, p, 0] = 32
    return {"x": x.reshape(N, 128, 4 * T), "u": u.reshape(N, 128, 512), **weights(rng, w.reshape(N, 128, 2048))}
def setup_inputs_borders(rng):
    c = np.ones((8, 16), int)
    for i, g in enumerate(rng.permutation(8)):
        e = rng.permutation(16)
        n = 16 if i < 2 else int(rng.integers(4, 17))
        c[g, e[0]] += n
        for k in rng.integers(1, 16, 16 - n): c[g, e[k]] += 1
    return signals(rng, np.stack([np.repeat(c, T // 16, axis=1)] * N))
def setup_inputs_stretches(rng):
    c, j = np.ones((N, 8, T), int), np.arange(T)
    for r in range(N):
        for g, k in enumerate(rng.permutation(8)):
            n = int(rng.integers(T // 8, T // 2))
            s = int(rng.integers(1, T - n))
            mid = (j >= s) & (j < s + n)
            loud = [j >= 0, j < 0, j == 0, j == T - 1, j < n, j >= T - n, ~mid, mid][int(k)]
            c[r, g, loud] = 17
    return signals(rng, c)
def setup_inputs_sizes(rng):
    d = setup_inputs(rng)
    small = np.arange(N) >> (L - 1) == int(rng.integers(0, 2))
    k = np.where(small, 2.0 ** -18, 2.0 ** -8).astype(np.float32)
    d["x"] = np.array(mx_ref.flush((d["x"].astype(np.float32) * k[:, None, None]).astype(BF)))
    for r in np.flatnonzero(~small & (np.arange(N) % 2 == int(rng.integers(0, 2)))):
        d["x"][r, :8] = ((1 - 2 * rng.integers(0, 2, (8, 4 * T))) * (1 + rng.random((8, 4 * T))) * 2.0 ** -29).astype(np.float32).astype(BF)
    u = (1 - 2 * rng.integers(0, 2, (N, 128, 128, 4))) * (1 + rng.random((N, 128, 128, 4))) * 2.0 ** rng.integers(-29, 29, (N, 1, 128, 1))
    i = np.arange(32)
    u[:, :, ::4] = 0
    u[:, i // 4, 4 * i, i % 4] = 2.0 ** -30
    d["u"] = u.astype(np.float32).astype(BF).reshape(N, 128, 512)
    return d
def setup_inputs_rests(rng):
    d = setup_inputs(rng)
    x = d["x"].reshape(N, 128, T, 4)
    for r in range(N):
        k = rng.permutation(T) % 3
        e = int(np.flatnonzero(k == 2)[0])
        x[r][:, k == 0] = 0
        x[r][:, k == 1] = x[r][:, e:e + 1]
    x[int(rng.integers(0, N))] = 0
    d["x"] = x.reshape(N, 128, 4 * T)
    return d
def setup_inputs_spread(rng):
    d = setup_inputs(rng)
    d["x"] = big(wide(rng, N, 128, 4 * T, cols=6), 1)
    return d
def check_inputs(d):
    b = []
    for k in ("x", "u"):
        v = np.abs(d[k].astype(np.float32))
        if not (np.isfinite(v).all() and ((v == 0) | (v >= 2.0 ** -30) & (v <= 2.0 ** 30)).all()): b.append("a value of " + k)
    return b
def reference(x, u, wc, ws):
    qu = [mx_ref.quantize(np.ascontiguousarray(u[r])) for r in range(N)]
    w = [pk(wc[r], ws[r]) for r in range(N)]
    t = [np.ascontiguousarray(x[r]) for r in range(N)]
    a = [mx_ref.quantize(t[r]) for r in range(N)]
    for b in range(R):
        phase, v = [], []
        for r in range(N):
            c, first, p = clock(mx_ref.matmul(qu[r], a[r]))
            phase.append(p)
            v.append(mx_ref.quantize(gcols(t[r], first)))
        d = decode(join(*a, *v))
        da, dv = d[:, :4 * N * T].reshape(8, 16, N, T, 4), d[:, 4 * N * T:].reshape(8, 16, N, M, 4)
        for r in range(N):
            q = r ^ (1 << (b % L))
            got = np.stack([dv[g, :, q][:, phase[r][g]] for g in range(8)])
            h = ((da[:, :, r] + got) * np.float32(0.5)).reshape(128, 4 * T).astype(BF)
            h = mx_ref.quantize(np.ascontiguousarray(h))
            t[r] = tile([mx_ref.matmul(pick(w[r], np.arange(128 * i, 128 * i + 128)), h) * np.float32(0.03125) for i in range(4)])
            a[r] = mx_ref.quantize(t[r])
    y, cl = np.zeros((N, 128, T), np.float32), np.zeros((N, 8, T), np.float32)
    oc, osc = np.zeros((N, 128, 4 * T), np.uint8), np.zeros((N, 16, T), np.uint8)
    for r in range(N):
        y[r] = mx_ref.matmul(qu[r], a[r])
        c, first, p = clock(y[r])
        cl[r] = c
        oc[r], osc[r] = emit(a[r])
    return {"y": y, "cl": cl, "oc": oc, "osc": osc}

@@ -1,0 +1,422 @@
+from concourse.mybir import dt, AluOpType as ALU, ActivationFunctionType as ACT
+
+TC, M, ROUNDS = 448, 128, 3
+NW = TC // 4
+NB = TC // 16
+CH = [(0, 192), (192, 320), (320, 448)]
+BIG = 1.0e6
+EPS = 2.0 ** -120
+MAGIC = 1.5 * 2.0 ** 23
+DELTA = 2.0 ** -14
+BF, F32, I32, U16, Q4, U8 = "bfloat16", "float32", "int32", "uint16", "float8_e4m3fn_x4", "uint8"
+
+SCRATCH = {}
+
+
+def _sb(name, n, dtype):
+    SCRATCH[name] = ("sbuf", [128, n], dtype)
+
+
+def _mx(name, n):
+    _sb(name + "q", n, Q4)
+    _sb(name + "s", n, U8)
+
+
+for _r in range(ROUNDS + 1):
+    _sb("t%d" % _r, 4 * TC, BF)
+    _mx("a%d" % _r, TC)
+for _r in range(ROUNDS):
+    _mx("v%d" % _r, M)
+    _mx("l%d" % _r, M)
+for _n, _w, _d in [("ut", 512, BF), ("et", 2048, BF), ("gt", 2048, BF), ("bt", 512, BF), ("ft", 512, BF), ("kt", 640, BF),
+                   ("bw", 4 * TC, BF), ("vt", 512, BF), ("ht", 4 * TC, BF), ("da", 4 * TC, BF), ("dv", 512, BF),
+                   ("dg", 4 * TC, BF), ("half", 512, BF), ("krow", 128, BF), ("yy", 128, BF), ("pi", 1, I32), ("ci", 4, I32),
+                   ("cf", 4, F32), ("cc", 4, F32), ("uu", 128, F32), ("nrow", 128, F32), ("kcol", 8, F32),
+                   ("ie", 32, F32), ("iw", NW, F32), ("me", 32, F32), ("mw", NW, F32), ("c36", NW, F32),
+                   ("c9", TC, BF), ("cw", 128, F32), ("cq", NW, F32), ("cs", NW, F32), ("ee", 32, F32),
+                   ("thr", 128, F32), ("thc", 8, F32), ("acc", 8, F32), ("junk", 8 * NB, BF), ("offb", 8, U16),
+                   ("offv", 32, U16), ("offp", NW, U16), ("rs", 1, F32), ("cx", NW, F32), ("p1", NW, F32),
+                   ("p2", NW, F32), ("yt", TC, F32), ("ct", TC, F32)]:
+    _sb(_n, _w, _d)
+for _n, _w in [("u", 128), ("w", 512), ("e", 512), ("g", 512), ("b", 128), ("f", 128), ("k", 160), ("h", TC), ("bw", TC)]:
+    _mx(_n + "_", _w)
+for _b in range(8):
+    SCRATCH["ps%d" % _b] = ("psum", [128, 512], F32)
+
+POOL = ["s%d" % _i for _i in range(140)]
+SEMAPHORES = POOL + ["arr%d" % _r for _r in range(ROUNDS)] + ["sent", "out"]
+
+
+def _plan(T, topo, core, rank):
+    ops = []
+
+    def view(name, lo=0, hi=None, step=1):
+        hi = SCRATCH[name][1][1] if hi is None else hi
+        bits = 0
+        if step == 1:
+            bits = ((1 << (hi - lo)) - 1) << lo
+        else:
+            for c in range(lo, hi, step):
+                bits |= 1 << c
+        ap = T[name][:, lo:hi] if step == 1 else T[name][:, lo:hi:step]
+        return (ap, name, bits)
+
+    def op(q, fn, reads, writes, group=None, acc=False, after=(), sem=None, dma=False):
+        ops.append({"q": q, "fn": fn, "r": [v for v in reads if isinstance(v, tuple)], "w": list(writes),
+                    "group": group, "acc": acc, "after": list(after), "sem": sem, "dma": dma})
+        return len(ops) - 1
+
+    def ap(v):
+        return v[0] if isinstance(v, tuple) else v
+
+    def memset(o, c, **k):
+        return op("v", lambda g: g.vector.memset(o[0], c), [], [o], **k)
+
+    def ts(o, i, s1, s2, o0, o1=None, **k):
+        if o1 is None:
+            return op("v", lambda g: g.vector.tensor_scalar(o[0], i[0], ap(s1), None, o0), [i, s1], [o], **k)
+        return op("v", lambda g: g.vector.tensor_scalar(o[0], i[0], ap(s1), ap(s2), o0, o1), [i, s1, s2], [o], **k)
+
+    def tt(o, a, b, alu, off=None, **k):
+        return op("v", lambda g: g.vector.tensor_tensor(o[0], a[0] if off is None else a[0].indirect(off[0]), b[0], alu),
+                  [a, b, off], [o], **k)
+
+    def vcopy(o, i, off=None, **k):
+        return op("v", lambda g: g.vector.tensor_copy(o[0], i[0] if off is None else i[0].indirect(off[0])),
+                  [i, off], [o], **k)
+
+    def scan(o, d0, d1, init, o0, o1, **k):
+        return op("v", lambda g: g.vector.tensor_tensor_scan(o[0], d0[0], d1[0], ap(init), o0, o1), [d0, d1, init], [o], **k)
+
+    def act(o, i, f, bias=0.0, scale=1.0, accum=None, off=None, **k):
+        def fn(g):
+            src = i[0] if off is None else i[0].indirect(off[0])
+            if accum is None:
+                return g.scalar.activation(o[0], src, f, bias=ap(bias), scale=ap(scale))
+            return g.scalar.activation(o[0], src, f, bias=ap(bias), scale=ap(scale), accum_out=accum[0])
+        return op("s", fn, [i, bias, scale, off], [o] + ([accum] if accum else []), **k)
+
+    def quant(name, lo, hi, src, slo, **k):
+        q, s, i = view(name + "q", lo, hi), view(name + "s", lo, hi), view(src, 4 * slo, 4 * (slo + hi - lo))
+        return op("v", lambda g: g.vector.quantize_mx(q[0], s[0], i[0]), [i], [q, s], **k)
+
+    def mm(bank, lname, l0, rname, r0, r1, start=True, stop=True, **k):
+        o = view("ps%d" % bank, 0, r1 - r0)
+        lq, ls = view(lname + "q", l0, l0 + 128), view(lname + "s", l0, l0 + 128)
+        rq, rsc = view(rname + "q", r0, r1), view(rname + "s", r0, r1)
+        return op("t", lambda g: g.tensor.matmul_mx(o[0], lq[0], ls[0], rq[0], rsc[0], start, stop),
+                  [lq, ls, rq, rsc], [o], acc=not start, **k)
+
+    def iota(o, pattern, cm=0):
+        if SCRATCH[o[1]][2] == I32:
+            return op("g", lambda g: g.iota(o[0], pattern, 0, cm), [], [o])
+        return op("g", lambda g: g.iota(o[0], pattern, 0, cm, allow_small_or_imprecise_dtypes=True), [], [o])
+
+    def load(q, o, src, code=False, **k):
+        dst = o[0].bitcast(dt.uint8) if code else o[0]
+        if q == "y":
+            return op("y", lambda g: g.sync.dma_start(dst, src), [], [o], dma=True, **k)
+        return op("s", lambda g: g.scalar.dma_start(dst, src), [], [o], dma=True, **k)
+
+    def store(q, dst, src, i):
+        if q == "y":
+            return op("y", lambda g: g.sync.dma_start(dst, src), [i], [], dma=True, sem="out")
+        return op("s", lambda g: g.scalar.dma_start(dst, src), [i], [], dma=True, sem="out")
+
+    G_TOT, G_SUF, G_F, G_C = 0, 1, 2, 3
+    col = lambda name, c: view(name, c, c + 1)
+    S = col("cw", NW - 1)
+    ECOL = col("cf", 2)
+    N0 = CH[0][1]
+
+    load("s", view("ut"), T.u[:, :])
+    last = None
+    for c0, c1 in CH:
+        last = load("y", view("t0", 4 * c0, 4 * c1), T.x[:, 4 * c0:4 * c1])
+    load("y", view("w_q"), T.wc[:, :], code=True, after=[last], group="w")
+    load("y", view("w_s"), T.ws[:, :], group="w")
+
+    iota(view("pi"), [[0, 1]], 1)
+    iota(view("uu"), [[-8, 8], [-1, 4], [0, 4]])
+    iota(view("nrow"), [[1, 128]])
+    iota(view("ie"), [[0, 2], [1, 16]])
+    iota(view("iw"), [[0, NB], [1, 4]])
+    memset(view("ft"), 0.0)
+    ts(col("ci", 0), view("pi"), 1, 0x38, ALU.logical_shift_right, ALU.bitwise_and, group="ci")
+    ts(col("ci", 1), view("pi"), 2, 3, ALU.logical_shift_right, ALU.bitwise_and, group="ci")
+    ts(col("ci", 2), view("pi"), 3, None, ALU.bitwise_and, group="ci")
+    ts(col("ci", 3), view("pi"), 15, None, ALU.bitwise_and, group="ci")
+    vcopy(view("cf"), view("ci"))
+    memset(view("half"), 0.5)
+    memset(view("bt", TC, 512), 0.0)
+    memset(view("cw", NW, 128), BIG)
+    act(view("yy"), view("uu"), ACT.Square, bias=col("cf", 0))
+    act(view("et", 1024, 1536), view("ft"), ACT.Identity, group="ez")
+    act(view("et", 1536, 2048), view("ft"), ACT.Identity, group="ez")
+    act(view("kt", 256, 640), view("ft", 0, 384), ACT.Identity)
+    for k in (G_F, G_TOT, G_SUF):
+        for t in range(4):
+            o = view("gt", 512 * k + t, 512 * k + 512, 4)
+            ts(o, view("yy"), 16.0 if k == G_TOT else float(t * t), 0.5, ALU.is_equal if k == G_F else ALU.is_lt, ALU.mult,
+               group="gf" if k == G_F else "g0")
+    quant("g_", 0, 384, "gt", 0)
+    act(view("gt", 512 * G_C, 512 * G_C + 512), view("gt", 512 * G_F, 512 * G_F + 512), ACT.Identity, scale=16.0)
+    act(col("cc", 3), col("cf", 3), ACT.Identity, scale=1.0 / 128)
+    act(view("krow"), view("nrow"), ACT.Identity, scale=1.0 / 128)
+    act(col("cc", 0), col("cf", 1), ACT.Identity, bias=27.0, scale=-9.0)
+    act(col("cc", 1), col("cf", 1), ACT.Identity, bias=36.0, scale=-9.0)
+    act(col("cc", 2), ECOL, ACT.Identity, bias=MAGIC, scale=-128.0)
+    act(view("kcol"), view("nrow", 0, 128, 16), ACT.Identity, bias=col("cc", 3), scale=1.0 / 128)
+    for b in (0, 1):
+        o, h = view("et", 512 * b, 512 * b + 512), view("half")
+        op("g", lambda g, o=o, h=h, b=b: g.affine_select(o[0], h[0], [[-4, 128], [-1, 4]], ALU.is_equal, 0.0, b, 4), [h], [o])
+    for b in (2, 3):
+        o, h = view("et", 512 * b + b, 512 * b + 512, 4), view("half", 0, 128)
+        op("g", lambda g, o=o, h=h: g.affine_select(o[0], h[0], [[-1, 128]], ALU.is_equal, 0.0, 0, 1), [h], [o])
+    quant("u_", 0, 128, "ut", 0)
+
+    def product_z(r, k):
+        mm(4 + k, "u_", 0, "a%d" % r, CH[k][0], CH[k][1])
+
+    def signs(r, k):
+        c0, c1 = CH[k]
+        if r < ROUNDS:
+            act(view("bt", c0, c1), view("ps%d" % (4 + k), 0, c1 - c0), ACT.Sign, bias=-EPS, group="sg%d" % r)
+        else:
+            act(view("bw", 4 * c0, 4 * c1, 4), view("ps%d" % (4 + k), 0, c1 - c0), ACT.Sign, bias=-EPS)
+
+    def clocks(r):
+        t, a = "t%d" % r, "a%d" % r
+        if r == 0:
+            memset(view("c36"), 36.0)
+            ts(view("me"), view("ie"), col("cf", 3), BIG, ALU.is_equal, ALU.mult)
+            ts(view("mw"), view("iw"), ECOL, BIG, ALU.is_equal, ALU.mult)
+            quant("g_", 384, 512, "gt", 384)
+        quant("b_", 0, 128, "bt", 0)
+        mm(7, "g_", 128 * G_TOT, "b_", 0, 128)
+        mm(4, "g_", 128 * G_SUF, "b_", 0, 128)
+        mm(5, "g_", 128 * G_F, "b_", 0, 128)
+        if r > 0:
+            mm(0, "e_", 0, a, 0, TC)
+            mm(1, "e_", 128, a, 0, TC)
+        scan(view("cw", 0, NW), view("ps7", 0, NW), view("c36"), 0.0, ALU.add, ALU.add)
+        act(view("thc"), view("kcol"), ACT.Identity, bias=1.0 / 256, scale=S)
+        for c in range(8):
+            act(view("junk", NB * c, NB * c + NB), view("cw", 3, NW, 4), ACT.Sign, bias=col("thc", c), scale=-1.0,
+                accum=col("acc", c), group="acc%d" % r)
+        if r > 0:
+            for b in range(2):
+                act(view("da", b, 4 * N0, 4), view("ps%d" % b, 0, N0), ACT.Copy, group="da%d" % r)
+        scan(view("ee"), view("me"), view("cw", 3, 128, 4), 0.0, ALU.max, ALU.min)
+        tt(view("cq"), view("cw", 0, NW), view("ps4", 0, NW), ALU.subtract)
+        ts(view("kt", 0, 128), view("krow"), S, col("ee", 15), ALU.mult, ALU.is_ge, group="kb%d" % r)
+        ts(view("kt", 128, 256), view("krow"), S, col("ee", 31), ALU.mult, ALU.is_ge, group="kb%d" % r)
+        scan(view("cs"), view("mw"), view("cq"), 0.0, ALU.max, ALU.min, group="fine%d" % r)
+        quant("k_", 0, 160, "kt", 0)
+        ts(view("thr"), view("krow"), S, col("cc", 0), ALU.mult, ALU.add, group="fine%d" % r)
+        mm(6, "g_", 128 * G_C, "k_", 0, 128, True, False, group="f%d" % r)
+        mm(6, "g_", 128 * G_C, "k_", 32, 160, False, False, group="f%d" % r)
+        ts(view("offb"), view("acc"), 2.0, float(2 * NB + 3), ALU.mult, ALU.add)
+        tt(view("ft", 0, 128), view("cs"), view("thr"), ALU.is_le, off=view("offb"))
+        quant("f_", 0, 128, "ft", 0)
+        mm(6, "g_", 128 * G_F, "f_", 0, 128, False, True, group="f%d" % r)
+        if r == 0:
+            quant("e_", 0, 128, "et", 0)
+        ts(view("offv"), view("ps6", 0, 32), 8.0, ECOL, ALU.mult, ALU.add)
+        vcopy(view("vt", 0, 256), view(t), off=view("offv", 0, 16), group="v%d" % r)
+        act(view("vt", 256, 512), view(t), ACT.Copy, off=view("offv", 16, 32), group="v%d" % r)
+        quant("v%d" % r, 0, M, "vt", 0)
+        dst = T.cores[rank ^ (1 << r)]
+        rid, pid = topo.addr(dst)[0], topo.addr(dst)[1]
+        mask = topo.mask(core, dst)
+        vq, vs, lq, ls = view("v%dq" % r), view("v%ds" % r), view("l%dq" % r), view("l%ds" % r)
+        arr = T.sem["arr%d" % r]
+        op("g", lambda g: g.remote_dma(lq[0].bitcast(dt.uint8), vq[0].bitcast(dt.uint8), arr, T.sem.sent, pid, rid, mask),
+           [vq], [], sem="remote")
+        op("g", lambda g: g.remote_dma(ls[0], vs[0], arr, T.sem.sent, pid, rid, mask), [vs], [], sem="remote")
+        n_eng = len(topo.engines(core, dst))
+        ops.append({"q": None, "fn": None, "r": [], "w": [lq, ls], "group": None, "acc": False, "after": [],
+                    "sem": ("arr%d" % r, 2 * n_eng), "dma": False})
+        if r == 0:
+            mm(0, "e_", 0, a, 0, TC)
+            for b in range(1, 4):
+                quant("e_", 128 * b, 128 * b + 128, "et", 128 * b)
+                mm(b, "e_", 128 * b, a, 0, TC)
+        else:
+            mm(2, "e_", 256, a, 0, TC)
+            mm(3, "e_", 384, a, 0, TC)
+        for b in range(0 if r == 0 else 2, 4):
+            act(view("da", b, 4 * N0, 4), view("ps%d" % b, 0, N0), ACT.Copy, group="da%d" % r)
+        op("v", lambda g: g.vector.reciprocal(view("rs")[0], S[0]), [S], [view("rs")], group="px%d" % r)
+        tt(view("cx"), view("cq"), view("ps5", 0, NW), ALU.subtract, group="px%d" % r)
+        ts(view("p1"), view("cx"), col("cc", 1), view("rs"), ALU.subtract, ALU.mult)
+        ts(view("p2"), view("p1"), 128.0, DELTA - 0.5, ALU.mult, ALU.add)
+        ts(view("offp"), view("p2"), MAGIC, col("cc", 2), ALU.add, ALU.subtract)
+        if r == 1:
+            memset(view("bw", 0, 2 * TC), 0.0)
+            memset(view("c9"), 9.0)
+        if r == 2:
+            memset(view("bw", 2 * TC, 4 * TC), 0.0)
+        return 2 * n_eng
+
+    def mix(r):
+        t, a = "t%d" % (r + 1), "a%d" % (r + 1)
+        for b in range(4):
+            mm(4 + b, "e_", 128 * b, "l%d" % r, 0, M)
+        for b in range(4):
+            o, i = view("dv", 128 * b, 128 * b + 128), view("ps%d" % (4 + b), 0, M)
+            if b % 2 == 1:
+                vcopy(o, i, group="dv%d" % r)
+            else:
+                act(o, i, ACT.Copy, group="dv%d" % r)
+        for c0, c1 in CH[1:]:
+            act(view("dg", 4 * c0, 4 * c1), view("dv"), ACT.Copy, off=view("offp", c0 // 4, c1 // 4))
+
+        def add(k, b):
+            c0, c1 = CH[k]
+            tt(view("ht", 4 * c0 + b, 4 * c1, 4), view("dg", 4 * c0 + b, 4 * c1, 4), view("ps%d" % b, c0, c1), ALU.add,
+               group="add%d_%d" % (r, k))
+
+        for k, (c0, c1) in enumerate(CH):
+            if k == 0:
+                tt(view("ht", 4 * c0, 4 * c1), view("dv"), view("da", 4 * c0, 4 * c1), ALU.add,
+                   off=view("offp", c0 // 4, c1 // 4))
+            else:
+                for b in range(k - 1, 4):
+                    add(k, b)
+                if k == 1:
+                    add(2, 0)
+            quant("h_", c0, c1, "ht", c0)
+            base = 0 if k == 2 else 4
+            for i in range(4):
+                mm(base + i, "w_", 128 * i, "h_", c0, c1)
+            if k == 2:
+                quant(a, CH[0][0], CH[0][1], t, CH[0][0])
+                product_z(r + 1, 0)
+            for i in range(4):
+                o, p = view(t, 4 * c0 + i, 4 * c1, 4), view("ps%d" % (base + i), 0, c1 - c0)
+                if k == 2:
+                    ts(o, p, 0.03125, None, ALU.mult, group="ev%d" % r)
+                else:
+                    act(o, p, ACT.Copy, scale=0.03125)
+        signs(r + 1, 0)
+        if r + 1 == ROUNDS:
+            act(view("yt", 0, N0), view("ps4", 0, N0), ACT.Copy)
+        for k in (1, 2):
+            quant(a, CH[k][0], CH[k][1], t, CH[k][0])
+            product_z(r + 1, k)
+            signs(r + 1, k)
+
+    def outputs():
+        a = "a%d" % ROUNDS
+        q = view(a + "q", 0, N0)
+        store("y", T.oc[:, 0:4 * N0], q[0].bitcast(dt.uint8), q)
+        q = view(a + "q", N0, TC)
+        store("y", T.oc[:, 4 * N0:4 * TC], q[0].bitcast(dt.uint8), q)
+        store("y", T.y[:, 0:N0], view("yt", 0, N0)[0], view("yt", 0, N0))
+        for k in range(4):
+            store("y", T.osc[4 * k:4 * k + 4, 0:TC], T[a + "s"][32 * k:32 * k + 4, 0:TC], view(a + "s"))
+        for k in (1, 2):
+            c0, c1 = CH[k]
+            act(view("yt", c0, c1), view("ps%d" % (4 + k), 0, c1 - c0), ACT.Copy, group="y")
+        store("s", T.y[:, N0:TC], view("yt", N0, TC)[0], view("yt", N0, TC))
+        for k, (c0, c1) in enumerate(CH):
+            quant("bw_", c0, c1, "bw", c0)
+            mm(k, "g_", 128 * G_TOT, "bw_", c0, c1)
+            if k > 0:
+                d0, d1 = CH[k - 1]
+                scan(view("ct", d0, d1), view("ps%d" % (k - 1), 0, d1 - d0), view("c9", d0, d1),
+                     col("ct", d0 - 1) if d0 else 0.0, ALU.add, ALU.add)
+        scan(view("ct", c0, c1), view("ps2", 0, c1 - c0), view("c9", c0, c1), col("ct", c0 - 1), ALU.add, ALU.add)
+        store("y", T.cl[:, :], T.ct[0:128:16, 0:TC], view("ct"))
+
+    for k, (c0, c1) in enumerate(CH):
+        quant("a0", c0, c1, "t0", c0)
+        product_z(0, k)
+        signs(0, k)
+    sent = 0
+    for r in range(ROUNDS):
+        sent += clocks(r)
+        mix(r)
+    outputs()
+    return ops, sent
+
+
+def _clash(x, y):
+    for xs, ys, both_read in ((x["w"], y["r"], False), (x["w"], y["w"], False), (x["r"], y["w"], False), (x["r"], y["r"], True)):
+        for a in xs:
+            for b in ys:
+                if a[1] != b[1]:
+                    continue
+                if a[1].startswith("ps"):
+                    if x["q"] != y["q"] or not (both_read or y["acc"]):
+                        return True
+                elif not both_read and a[2] & b[2]:
+                    return True
+    return False
+
+
+def _emit(g, T, ops, sent):
+    members = {}
+    for n, o in enumerate(ops):
+        o["tok"] = o["group"] or ("#%d" % n)
+        members.setdefault(o["tok"], []).append(n)
+    known = {q: set() for q in "gvsty"}
+    waited = []
+    for n, o in enumerate(ops):
+        o["waits"] = []
+        if o["q"] is None:
+            o["snap"] = set()
+            continue
+        k = known[o["q"]]
+        for m in range(n - 1, -1, -1):
+            if m in k or not (m in o["after"] or _clash(ops[m], o)):
+                continue
+            tok = ops[m]["tok"]
+            assert tok != o["tok"] and members[tok][-1] < n, (tok, n)
+            o["waits"].append(tok)
+            if tok not in waited:
+                waited.append(tok)
+            for j in members[tok]:
+                k.add(j)
+                k |= ops[j]["snap"]
+        o["snap"] = set(k)
+    sem_of, state, fresh = {}, {}, list(POOL)
+    for tok in sorted(waited, key=lambda t: members[t][0]):
+        mem = members[tok]
+        first = ops[mem[0]]
+        if first["q"] is None:
+            sem_of[tok] = first["sem"]
+            continue
+        assert first["sem"] is None
+        inc = sum(16 if ops[j]["dma"] else 1 for j in mem)
+        if fresh:
+            name = fresh.pop(0)
+            state[name] = [0, []]
+        else:
+            name = [s for s in POOL if all(p in ops[j]["snap"] for p in state[s][1] for j in mem)][0]
+        state[name] = [state[name][0] + inc, mem]
+        sem_of[tok] = (name, state[name][0])
+    queue = {"g": g, "v": g.vector, "s": g.scalar, "t": g.tensor, "y": g.sync}
+    outs = 0
+    for o in ops:
+        if o["q"] is None:
+            continue
+        for tok in o["waits"]:
+            queue[o["q"]].wait_ge(T.sem[sem_of[tok][0]], sem_of[tok][1])
+        ins = o["fn"](g)
+        if o["sem"] == "out":
+            ins.then_inc(T.sem.out, 16)
+            outs += 16
+        elif o["tok"] in sem_of:
+            ins.then_inc(T.sem[sem_of[o["tok"]][0]], 16 if o["dma"] else 1)
+    g.wait_ge(T.sem.sent, sent)
+    g.sync.wait_ge(T.sem.out, outs)
+
+
+def rank_program(g, core, T, topo):
+    rank = T.rank_of(core)
+    if rank is None:
+        return
+    ops, sent = _plan(T, topo, core, rank)
+    _emit(g, T, ops, sent)

@@ -3,7 +3,7 @@ from concourse.mybir import dt, AluOpType as ALU, ActivationFunctionType as ACT
 TC, M, ROUNDS = 448, 128, 3
 NW = TC // 4
 NB = TC // 16
-CH = [(0, 192), (192, 320), (320, 448)]
+CH = [(0, 176), (176, 320), (320, 448)]
 BIG = 1.0e6
 EPS = 2.0 ** -120
 MAGIC = 1.5 * 2.0 ** 23
@@ -31,7 +31,7 @@ for _r in range(ROUNDS):
 for _n, _w, _d in [("ut", 512, BF), ("et", 2048, BF), ("gt", 2048, BF), ("bt", 512, BF), ("ft", 512, BF), ("kt", 640, BF),
                    ("bw", 4 * TC, BF), ("vt", 512, BF), ("ht", 4 * TC, BF), ("da", 4 * TC, BF), ("dv", 512, BF),
                    ("dg", 4 * TC, BF), ("half", 512, BF), ("krow", 128, BF), ("yy", 128, BF), ("pi", 1, I32), ("ci", 4, I32),
-                   ("cf", 4, F32), ("cc", 4, F32), ("uu", 128, F32), ("nrow", 128, F32), ("kcol", 8, F32),
+                   ("cf", 4, F32), ("cc", 6, F32), ("uu", 128, F32), ("nrow", 128, F32), ("kcol", 8, F32),
                    ("ie", 32, F32), ("iw", NW, F32), ("me", 32, F32), ("mw", NW, F32), ("c36", NW, F32),
                    ("c9", TC, BF), ("cw", 128, F32), ("cq", NW, F32), ("cs", NW, F32), ("ee", 32, F32),
                    ("thr", 128, F32), ("thc", 8, F32), ("acc", 8, F32), ("junk", 8 * NB, BF), ("offb", 8, U16),
@@ -128,6 +128,7 @@ def _plan(T, topo, core, rank):
     S = col("cw", NW - 1)
     ECOL = col("cf", 2)
     N0 = CH[0][1]
+    W2 = CH[2][0] // 4
 
     load("s", view("ut"), T.u[:, :])
     last = None
@@ -136,63 +137,41 @@ def _plan(T, topo, core, rank):
     load("y", view("w_q"), T.wc[:, :], code=True, after=[last], group="w")
     load("y", view("w_s"), T.ws[:, :], group="w")
 
-    iota(view("pi"), [[0, 1]], 1)
-    iota(view("uu"), [[-8, 8], [-1, 4], [0, 4]])
-    iota(view("nrow"), [[1, 128]])
-    iota(view("ie"), [[0, 2], [1, 16]])
-    iota(view("iw"), [[0, NB], [1, 4]])
-    memset(view("ft"), 0.0)
-    ts(col("ci", 0), view("pi"), 1, 0x38, ALU.logical_shift_right, ALU.bitwise_and, group="ci")
-    ts(col("ci", 1), view("pi"), 2, 3, ALU.logical_shift_right, ALU.bitwise_and, group="ci")
-    ts(col("ci", 2), view("pi"), 3, None, ALU.bitwise_and, group="ci")
-    ts(col("ci", 3), view("pi"), 15, None, ALU.bitwise_and, group="ci")
-    vcopy(view("cf"), view("ci"))
-    memset(view("half"), 0.5)
-    memset(view("bt", TC, 512), 0.0)
-    memset(view("cw", NW, 128), BIG)
-    act(view("yy"), view("uu"), ACT.Square, bias=col("cf", 0))
-    act(view("et", 1024, 1536), view("ft"), ACT.Identity, group="ez")
-    act(view("et", 1536, 2048), view("ft"), ACT.Identity, group="ez")
-    act(view("kt", 256, 640), view("ft", 0, 384), ACT.Identity)
-    for k in (G_F, G_TOT, G_SUF):
-        for t in range(4):
-            o = view("gt", 512 * k + t, 512 * k + 512, 4)
-            ts(o, view("yy"), 16.0 if k == G_TOT else float(t * t), 0.5, ALU.is_equal if k == G_F else ALU.is_lt, ALU.mult,
-               group="gf" if k == G_F else "g0")
-    quant("g_", 0, 384, "gt", 0)
-    act(view("gt", 512 * G_C, 512 * G_C + 512), view("gt", 512 * G_F, 512 * G_F + 512), ACT.Identity, scale=16.0)
-    act(col("cc", 3), col("cf", 3), ACT.Identity, scale=1.0 / 128)
-    act(view("krow"), view("nrow"), ACT.Identity, scale=1.0 / 128)
-    act(col("cc", 0), col("cf", 1), ACT.Identity, bias=27.0, scale=-9.0)
-    act(col("cc", 1), col("cf", 1), ACT.Identity, bias=36.0, scale=-9.0)
-    act(col("cc", 2), ECOL, ACT.Identity, bias=MAGIC, scale=-128.0)
-    act(view("kcol"), view("nrow", 0, 128, 16), ACT.Identity, bias=col("cc", 3), scale=1.0 / 128)
-    for b in (0, 1):
-        o, h = view("et", 512 * b, 512 * b + 512), view("half")
-        op("g", lambda g, o=o, h=h, b=b: g.affine_select(o[0], h[0], [[-4, 128], [-1, 4]], ALU.is_equal, 0.0, b, 4), [h], [o])
-    for b in (2, 3):
-        o, h = view("et", 512 * b + b, 512 * b + 512, 4), view("half", 0, 128)
-        op("g", lambda g, o=o, h=h: g.affine_select(o[0], h[0], [[-1, 128]], ALU.is_equal, 0.0, 0, 1), [h], [o])
-    quant("u_", 0, 128, "ut", 0)
-
     def product_z(r, k):
         mm(4 + k, "u_", 0, "a%d" % r, CH[k][0], CH[k][1])
 
     def signs(r, k):
         c0, c1 = CH[k]
-        if r < ROUNDS:
-            act(view("bt", c0, c1), view("ps%d" % (4 + k), 0, c1 - c0), ACT.Sign, bias=-EPS, group="sg%d" % r)
+        o = view("bt", c0, c1) if r < ROUNDS else view("bw", 4 * c0, 4 * c1, 4)
+        z = view("ps%d" % (4 + k), 0, c1 - c0)
+        if k == 2:
+            ts(o, z, 0.0, 2.0, ALU.is_gt, ALU.mult)
+        elif r < ROUNDS:
+            act(o, z, ACT.Sign, bias=-EPS, group="sg%d" % r)
         else:
-            act(view("bw", 4 * c0, 4 * c1, 4), view("ps%d" % (4 + k), 0, c1 - c0), ACT.Sign, bias=-EPS)
+            act(o, z, ACT.Sign, bias=-EPS)
 
-    def clocks(r):
+    def send(r, src, lo, hi):
+        dst = T.cores[rank ^ (1 << r)]
+        rid, pid = topo.addr(dst)[0], topo.addr(dst)[1]
+        mask = topo.mask(core, dst)
+        vq, vs, lq, ls = view(src + "q", lo, hi), view(src + "s", lo, hi), view("l%dq" % r, lo, hi), view("l%ds" % r, lo, hi)
+        arr = T.sem["arr%d" % r]
+        op("g", lambda g: g.remote_dma(lq[0].bitcast(dt.uint8), vq[0].bitcast(dt.uint8), arr, T.sem.sent, pid, rid, mask),
+           [vq], [], sem="remote")
+        op("g", lambda g: g.remote_dma(ls[0], vs[0], arr, T.sem.sent, pid, rid, mask), [vs], [], sem="remote")
+        return 2 * len(topo.engines(core, dst))
+
+    def clocks(r, head):
         t, a = "t%d" % r, "a%d" % r
-        if r == 0:
-            memset(view("c36"), 36.0)
-            ts(view("me"), view("ie"), col("cf", 3), BIG, ALU.is_equal, ALU.mult)
-            ts(view("mw"), view("iw"), ECOL, BIG, ALU.is_equal, ALU.mult)
-            quant("g_", 384, 512, "gt", 384)
+
+        def per_step():
+            op("v", lambda g: g.vector.reciprocal(view("rs")[0], S[0]), [S], [view("rs")], group="px%d" % r)
+            tt(view("cx"), view("cq"), view("ps5", 0, NW), ALU.subtract, group="px%d" % r)
+
         quant("b_", 0, 128, "bt", 0)
+        if r == 0:
+            quant("g_", 128, 384, "gt", 128)
         mm(7, "g_", 128 * G_TOT, "b_", 0, 128)
         mm(4, "g_", 128 * G_SUF, "b_", 0, 128)
         mm(5, "g_", 128 * G_F, "b_", 0, 128)
@@ -200,6 +179,8 @@ def _plan(T, topo, core, rank):
             mm(0, "e_", 0, a, 0, TC)
             mm(1, "e_", 128, a, 0, TC)
         scan(view("cw", 0, NW), view("ps7", 0, NW), view("c36"), 0.0, ALU.add, ALU.add)
+        if r == 0:
+            memset(view("kt", 256, 640), 0.0)
         act(view("thc"), view("kcol"), ACT.Identity, bias=1.0 / 256, scale=S)
         for c in range(8):
             act(view("junk", NB * c, NB * c + NB), view("cw", 3, NW, 4), ACT.Sign, bias=col("thc", c), scale=-1.0,
@@ -210,10 +191,16 @@ def _plan(T, topo, core, rank):
         scan(view("ee"), view("me"), view("cw", 3, 128, 4), 0.0, ALU.max, ALU.min)
         tt(view("cq"), view("cw", 0, NW), view("ps4", 0, NW), ALU.subtract)
         ts(view("kt", 0, 128), view("krow"), S, col("ee", 15), ALU.mult, ALU.is_ge, group="kb%d" % r)
+        ts(view("cq", W2, NW), view("cq", W2, NW), col("cc", 4), None, ALU.add)
         ts(view("kt", 128, 256), view("krow"), S, col("ee", 31), ALU.mult, ALU.is_ge, group="kb%d" % r)
         scan(view("cs"), view("mw"), view("cq"), 0.0, ALU.max, ALU.min, group="fine%d" % r)
         quant("k_", 0, 160, "kt", 0)
         ts(view("thr"), view("krow"), S, col("cc", 0), ALU.mult, ALU.add, group="fine%d" % r)
+        if r == 0:
+            quant("g_", 384, 512, "gt", 384)
+            act(col("cc", 1), col("cf", 1), ACT.Identity, bias=36.0, scale=-9.0)
+            act(col("cc", 5), col("cf", 1), ACT.Identity, bias=28.0, scale=-9.0)
+            act(col("cc", 2), ECOL, ACT.Identity, bias=MAGIC, scale=-128.0)
         mm(6, "g_", 128 * G_C, "k_", 0, 128, True, False, group="f%d" % r)
         mm(6, "g_", 128 * G_C, "k_", 32, 160, False, False, group="f%d" % r)
         ts(view("offb"), view("acc"), 2.0, float(2 * NB + 3), ALU.mult, ALU.add)
@@ -221,43 +208,41 @@ def _plan(T, topo, core, rank):
         quant("f_", 0, 128, "ft", 0)
         mm(6, "g_", 128 * G_F, "f_", 0, 128, False, True, group="f%d" % r)
         if r == 0:
-            quant("e_", 0, 128, "et", 0)
+            quant("e_", 0, 256, "et", 0)
+        else:
+            per_step()
         ts(view("offv"), view("ps6", 0, 32), 8.0, ECOL, ALU.mult, ALU.add)
         vcopy(view("vt", 0, 256), view(t), off=view("offv", 0, 16), group="v%d" % r)
         act(view("vt", 256, 512), view(t), ACT.Copy, off=view("offv", 16, 32), group="v%d" % r)
         quant("v%d" % r, 0, M, "vt", 0)
-        dst = T.cores[rank ^ (1 << r)]
-        rid, pid = topo.addr(dst)[0], topo.addr(dst)[1]
-        mask = topo.mask(core, dst)
-        vq, vs, lq, ls = view("v%dq" % r), view("v%ds" % r), view("l%dq" % r), view("l%ds" % r)
-        arr = T.sem["arr%d" % r]
-        op("g", lambda g: g.remote_dma(lq[0].bitcast(dt.uint8), vq[0].bitcast(dt.uint8), arr, T.sem.sent, pid, rid, mask),
-           [vq], [], sem="remote")
-        op("g", lambda g: g.remote_dma(ls[0], vs[0], arr, T.sem.sent, pid, rid, mask), [vs], [], sem="remote")
-        n_eng = len(topo.engines(core, dst))
-        ops.append({"q": None, "fn": None, "r": [], "w": [lq, ls], "group": None, "acc": False, "after": [],
-                    "sem": ("arr%d" % r, 2 * n_eng), "dma": False})
+        n_inc = head + send(r, "v%d" % r, 1 if head else 0, M)
+        ops.append({"q": None, "fn": None, "r": [], "w": [view("l%dq" % r), view("l%ds" % r)], "group": None, "acc": False,
+                    "after": [], "sem": ("arr%d" % r, n_inc), "dma": False})
         if r == 0:
             mm(0, "e_", 0, a, 0, TC)
-            for b in range(1, 4):
-                quant("e_", 128 * b, 128 * b + 128, "et", 128 * b)
-                mm(b, "e_", 128 * b, a, 0, TC)
-        else:
-            mm(2, "e_", 256, a, 0, TC)
-            mm(3, "e_", 384, a, 0, TC)
+            mm(1, "e_", 128, a, 0, TC)
+            quant("e_", 256, 512, "et", 256)
+        mm(2, "e_", 256, a, 0, TC)
+        mm(3, "e_", 384, a, 0, TC)
+        if r == 0:
+            per_step()
         for b in range(0 if r == 0 else 2, 4):
             act(view("da", b, 4 * N0, 4), view("ps%d" % b, 0, N0), ACT.Copy, group="da%d" % r)
-        op("v", lambda g: g.vector.reciprocal(view("rs")[0], S[0]), [S], [view("rs")], group="px%d" % r)
-        tt(view("cx"), view("cq"), view("ps5", 0, NW), ALU.subtract, group="px%d" % r)
-        ts(view("p1"), view("cx"), col("cc", 1), view("rs"), ALU.subtract, ALU.mult)
+        ts(view("p1", 0, W2), view("cx", 0, W2), col("cc", 1), view("rs"), ALU.subtract, ALU.mult, group="p1%d" % r)
+        ts(view("p1", W2, NW), view("cx", W2, NW), col("cc", 5), view("rs"), ALU.subtract, ALU.mult, group="p1%d" % r)
         ts(view("p2"), view("p1"), 128.0, DELTA - 0.5, ALU.mult, ALU.add)
         ts(view("offp"), view("p2"), MAGIC, col("cc", 2), ALU.add, ALU.subtract)
         if r == 1:
             memset(view("bw", 0, 2 * TC), 0.0)
-            memset(view("c9"), 9.0)
+            memset(view("c9", 0, CH[2][0]), 9.0)
+            memset(view("c9", CH[2][0], TC), 1.0)
         if r == 2:
             memset(view("bw", 2 * TC, 4 * TC), 0.0)
-        return 2 * n_eng
+        return n_inc
+
+    def steps(k):
+        quant("bw_", CH[k][0], CH[k][1], "bw", CH[k][0])
+        mm(k, "g_", 128 * G_TOT, "bw_", CH[k][0], CH[k][1])
 
     def mix(r):
         t, a = "t%d" % (r + 1), "a%d" % (r + 1)
@@ -295,7 +280,7 @@ def _plan(T, topo, core, rank):
                 product_z(r + 1, 0)
             for i in range(4):
                 o, p = view(t, 4 * c0 + i, 4 * c1, 4), view("ps%d" % (base + i), 0, c1 - c0)
-                if k == 2:
+                if k == 2 and i < 3:
                     ts(o, p, 0.03125, None, ALU.mult, group="ev%d" % r)
                 else:
                     act(o, p, ACT.Copy, scale=0.03125)
@@ -305,6 +290,8 @@ def _plan(T, topo, core, rank):
         for k in (1, 2):
             quant(a, CH[k][0], CH[k][1], t, CH[k][0])
             product_z(r + 1, k)
+            if k == 2 and r + 1 == ROUNDS:
+                steps(0)
             signs(r + 1, k)
 
     def outputs():
@@ -320,23 +307,73 @@ def _plan(T, topo, core, rank):
             c0, c1 = CH[k]
             act(view("yt", c0, c1), view("ps%d" % (4 + k), 0, c1 - c0), ACT.Copy, group="y")
         store("s", T.y[:, N0:TC], view("yt", N0, TC)[0], view("yt", N0, TC))
+        steps(1)
+        steps(2)
         for k, (c0, c1) in enumerate(CH):
-            quant("bw_", c0, c1, "bw", c0)
-            mm(k, "g_", 128 * G_TOT, "bw_", c0, c1)
-            if k > 0:
-                d0, d1 = CH[k - 1]
-                scan(view("ct", d0, d1), view("ps%d" % (k - 1), 0, d1 - d0), view("c9", d0, d1),
-                     col("ct", d0 - 1) if d0 else 0.0, ALU.add, ALU.add)
-        scan(view("ct", c0, c1), view("ps2", 0, c1 - c0), view("c9", c0, c1), col("ct", c0 - 1), ALU.add, ALU.add)
+            scan(view("ct", c0, c1), view("ps%d" % k, 0, c1 - c0), view("c9", c0, c1),
+                 col("ct", c0 - 1) if c0 else 0.0, ALU.add, ALU.add)
         store("y", T.cl[:, :], T.ct[0:128:16, 0:TC], view("ct"))
 
-    for k, (c0, c1) in enumerate(CH):
-        quant("a0", c0, c1, "t0", c0)
+    def gtile(k):
+        for t in range(4):
+            o = view("gt", 512 * k + t, 512 * k + 512, 4)
+            ts(o, view("yy"), 16.0 if k == G_TOT else float(t * t), 0.5, ALU.is_equal if k == G_F else ALU.is_lt, ALU.mult,
+               group="gt%d" % k)
+
+    def etile(b):
+        o, h = view("et", 512 * b, 512 * b + 512), view("half")
+        op("g", lambda g: g.affine_select(o[0], h[0], [[-4, 128], [-1, 4]], ALU.is_equal, 0.0, b, 4), [h], [o])
+
+    def first(k):
+        quant("a0", CH[k][0], CH[k][1], "t0", CH[k][0])
         product_z(0, k)
-        signs(0, k)
+
+    iota(view("pi"), [[0, 1]], 1)
+    iota(view("uu"), [[-8, 8], [-1, 4], [0, 4]])
+    iota(view("nrow"), [[1, 128]])
+    iota(view("ie"), [[0, 2], [1, 16]])
+    iota(view("iw"), [[0, NB], [1, 4]])
+    memset(view("ft"), 0.0)
+    ts(col("ci", 0), view("pi"), 1, 0x38, ALU.logical_shift_right, ALU.bitwise_and, group="ci")
+    ts(col("ci", 1), view("pi"), 2, 3, ALU.logical_shift_right, ALU.bitwise_and, group="ci")
+    ts(col("ci", 2), view("pi"), 3, None, ALU.bitwise_and, group="ci")
+    ts(col("ci", 3), view("pi"), 15, None, ALU.bitwise_and, group="ci")
+    memset(view("bt", TC, 512), 0.0)
+    vcopy(view("cf"), view("ci"))
+    memset(view("half"), 0.5)
+    memset(view("c36", 0, W2), 36.0, group="c36")
+    memset(view("c36", W2, NW), 4.0, group="c36")
+    act(view("et", 1536, 2048), view("ft"), ACT.Identity)
+    act(view("yy"), view("uu"), ACT.Square, bias=col("cf", 0))
+    act(col("cc", 3), col("cf", 3), ACT.Identity, scale=1.0 / 128)
+    act(view("krow"), view("nrow"), ACT.Identity, scale=1.0 / 128)
+    act(view("kcol"), view("nrow", 0, 128, 16), ACT.Identity, bias=col("cc", 3), scale=1.0 / 128)
+    act(col("cc", 0), col("cf", 1), ACT.Identity, bias=27.0, scale=-9.0)
+    act(col("cc", 4), col("cf", 1), ACT.Identity, bias=24.0, scale=-8.0)
+    etile(0)
+    memset(view("cw", NW, 128), BIG)
+    ts(view("me"), view("ie"), col("cf", 3), BIG, ALU.is_equal, ALU.mult)
+    gtile(G_TOT)
+    quant("u_", 0, 128, "ut", 0)
+    quant("g_", 0, 128, "gt", 0)
+    first(0)
+    signs(0, 0)
+    head = send(0, "a0", 0, 1)
+    etile(1)
+    etile(2)
+    o3, h3 = view("et", 1539, 2048, 4), view("half", 0, 128)
+    op("g", lambda g: g.affine_select(o3[0], h3[0], [[-1, 128]], ALU.is_equal, 0.0, 0, 1), [h3], [o3])
+    gtile(G_SUF)
+    first(1)
+    signs(0, 1)
+    gtile(G_F)
+    first(2)
+    ts(view("mw"), view("iw"), ECOL, BIG, ALU.is_equal, ALU.mult)
+    signs(0, 2)
+    act(view("gt", 512 * G_C, 512 * G_C + 512), view("gt", 512 * G_F, 512 * G_F + 512), ACT.Identity, scale=16.0)
     sent = 0
     for r in range(ROUNDS):
-        sent += clocks(r)
+        sent += clocks(r, head if r == 0 else 0)
         mix(r)
     outputs()
     return ops, sent

@@ -3,12 +3,42 @@ from concourse.mybir import dt, AluOpType as ALU, ActivationFunctionType as ACT
 TC, M, ROUNDS = 448, 128, 3
 NW = TC // 4
 NB = TC // 16
-CH = [(0, 176), (176, 320), (320, 448)]
 BIG = 1.0e6
 EPS = 2.0 ** -120
 MAGIC = 1.5 * 2.0 ** 23
 DELTA = 2.0 ** -14
+WIDE = 1.0 + 2.0 ** -21
+E0 = 1020
+FT, KT, BT = 0, 128, 384
 BF, F32, I32, U16, Q4, U8 = "bfloat16", "float32", "int32", "uint16", "float8_e4m3fn_x4", "uint8"
+
+CFG = {
+    "ld": [(0, 176), (176, 320), (320, 448)],
+    "thr": "s",
+    "grp": False,
+    "whole": 2,
+    "pieces": [160, 320, 448],
+    "start": "hf bz qu a0 me mw gt gs a1 q0 a2 rc gf",
+}
+
+
+def schedule(c1, c2, order, last, ev="ssss ssss vvvs"):
+    ch, ev = [(0, c1), (c1, c2), (c2, TC), (0, c2), (0, TC), (c1, TC)], ev.split()
+
+    def calls(text):
+        out = []
+        for step in text.split():
+            head, _, arg = step.partition(":")
+            kind, k = head[:-1], int(head[-1])
+            bank = {"h": (4, 4, 0), "e": (4, 4, 0), "b": (0, 1, 2, 0), "c": (0, 1, 2, 0)}.get(kind, (4, 5, 6, 4, 0, 0))[k]
+            out.append((kind, ch[k][0], ch[k][1], bank, arg or (ev[k] if kind == "e" else "")))
+        return out
+    CFG.update(da=c1, mix=calls(order), last=calls(last))
+
+
+schedule(160, 320, "G1 G2 g0 p1:0 h0 e0 p1:123 p2:0 h1 e1 p2:123 h2 a0 e2 s0 a1 a2 s1 s2",
+         "G1 G2 g0 p1:0 h0 e0 p1:123 p2:0 h1 e1 p2:123 h2 a0 e2 s0 oc0:y y0:s oy0:y a1 a2 oc5:y os4:yyyy "
+         "s1 s2 b0 b1 c0 b2 c1 c2 cl4:y y1:s y2:s oy5:s")
 
 SCRATCH = {}
 
@@ -28,23 +58,24 @@ for _r in range(ROUNDS + 1):
 for _r in range(ROUNDS):
     _mx("v%d" % _r, M)
     _mx("l%d" % _r, M)
-for _n, _w, _d in [("ut", 512, BF), ("et", 2048, BF), ("gt", 2048, BF), ("bt", 512, BF), ("ft", 512, BF), ("kt", 640, BF),
+for _n, _w, _d in [("ut", 512, BF), ("et", 516, BF), ("gt", 2048, BF), ("bk", BT + 512, BF), ("sq", 512, BF),
                    ("bw", 4 * TC, BF), ("vt", 512, BF), ("ht", 4 * TC, BF), ("da", 4 * TC, BF), ("dv", 512, BF),
-                   ("dg", 4 * TC, BF), ("half", 512, BF), ("krow", 128, BF), ("yy", 128, BF), ("pi", 1, I32), ("ci", 4, I32),
-                   ("cf", 4, F32), ("cc", 6, F32), ("uu", 128, F32), ("nrow", 128, F32), ("kcol", 8, F32),
+                   ("dg", 4 * TC, BF), ("krow", 128, BF), ("nkrow", 128, F32), ("pf", 2, F32), ("gh", 2, BF),
+                   ("cc", 8, F32), ("b4", 4, F32), ("uu", 128, F32), ("nrow", 128, F32), ("kcol", 8, F32),
                    ("ie", 32, F32), ("iw", NW, F32), ("me", 32, F32), ("mw", NW, F32), ("c36", NW, F32),
                    ("c9", TC, BF), ("cw", 128, F32), ("cq", NW, F32), ("cs", NW, F32), ("ee", 32, F32),
                    ("thr", 128, F32), ("thc", 8, F32), ("acc", 8, F32), ("junk", 8 * NB, BF), ("offb", 8, U16),
-                   ("offv", 32, U16), ("offp", NW, U16), ("rs", 1, F32), ("cx", NW, F32), ("p1", NW, F32),
-                   ("p2", NW, F32), ("yt", TC, F32), ("ct", TC, F32)]:
+                   ("offv", 32, U16), ("offp", NW, U16), ("rs", 1, F32), ("p1", NW, F32),
+                   ("p2", NW, F32), ("yt", TC, F32), ("ct", TC, F32), ("dw", 4 * TC, BF), ("offw", 32, U16)]:
     _sb(_n, _w, _d)
+_mx("lw", TC)
 for _n, _w in [("u", 128), ("w", 512), ("e", 512), ("g", 512), ("b", 128), ("f", 128), ("k", 160), ("h", TC), ("bw", TC)]:
     _mx(_n + "_", _w)
 for _b in range(8):
     SCRATCH["ps%d" % _b] = ("psum", [128, 512], F32)
 
 POOL = ["s%d" % _i for _i in range(140)]
-SEMAPHORES = POOL + ["arr%d" % _r for _r in range(ROUNDS)] + ["sent", "out"]
+SEMAPHORES = POOL + ["arr%d" % _r for _r in range(ROUNDS)] + ["arw", "sent", "out"]
 
 
 def _plan(T, topo, core, rank):
@@ -88,6 +119,9 @@ def _plan(T, topo, core, rank):
     def scan(o, d0, d1, init, o0, o1, **k):
         return op("v", lambda g: g.vector.tensor_tensor_scan(o[0], d0[0], d1[0], ap(init), o0, o1), [d0, d1, init], [o], **k)
 
+    def recip(o, i, **k):
+        return op("v", lambda g: g.vector.reciprocal(o[0], i[0]), [i], [o], **k)
+
     def act(o, i, f, bias=0.0, scale=1.0, accum=None, off=None, **k):
         def fn(g):
             src = i[0] if off is None else i[0].indirect(off[0])
@@ -96,8 +130,8 @@ def _plan(T, topo, core, rank):
             return g.scalar.activation(o[0], src, f, bias=ap(bias), scale=ap(scale), accum_out=accum[0])
         return op("s", fn, [i, bias, scale, off], [o] + ([accum] if accum else []), **k)
 
-    def quant(name, lo, hi, src, slo, **k):
-        q, s, i = view(name + "q", lo, hi), view(name + "s", lo, hi), view(src, 4 * slo, 4 * (slo + hi - lo))
+    def quant(name, lo, hi, src, first, **k):
+        q, s, i = view(name + "q", lo, hi), view(name + "s", lo, hi), view(src, first, first + 4 * (hi - lo))
         return op("v", lambda g: g.vector.quantize_mx(q[0], s[0], i[0]), [i], [q, s], **k)
 
     def mm(bank, lname, l0, rname, r0, r1, start=True, stop=True, **k):
@@ -107,10 +141,8 @@ def _plan(T, topo, core, rank):
         return op("t", lambda g: g.tensor.matmul_mx(o[0], lq[0], ls[0], rq[0], rsc[0], start, stop),
                   [lq, ls, rq, rsc], [o], acc=not start, **k)
 
-    def iota(o, pattern, cm=0):
-        if SCRATCH[o[1]][2] == I32:
-            return op("g", lambda g: g.iota(o[0], pattern, 0, cm), [], [o])
-        return op("g", lambda g: g.iota(o[0], pattern, 0, cm, allow_small_or_imprecise_dtypes=True), [], [o])
+    def iota(o, pattern, base=0, cm=0):
+        return op("g", lambda g: g.iota(o[0], pattern, base, cm, allow_small_or_imprecise_dtypes=True), [], [o])
 
     def load(q, o, src, code=False, **k):
         dst = o[0].bitcast(dt.uint8) if code else o[0]
@@ -123,260 +155,260 @@ def _plan(T, topo, core, rank):
             return op("y", lambda g: g.sync.dma_start(dst, src), [i], [], dma=True, sem="out")
         return op("s", lambda g: g.scalar.dma_start(dst, src), [i], [], dma=True, sem="out")
 
-    G_TOT, G_SUF, G_F, G_C = 0, 1, 2, 3
+    G_TOT, G_REST, G_F, G_C = 0, 1, 2, 3
+    B_Z, B_TOT, B_REST, B_F = 4, 6, 7, 4
     col = lambda name, c: view(name, c, c + 1)
     S = col("cw", NW - 1)
-    ECOL = col("cf", 2)
-    N0 = CH[0][1]
-    W2 = CH[2][0] // 4
+    C_E, C_I, C_A, C_MAGIC, C_G, C_K, C_T = [col("cc", c) for c in range(7)]
+    LD, WHOLE, count = CFG["ld"], CFG["whole"], {}
+    wide = lambda c0, c1: min(c0, c1 - 128)
 
     load("s", view("ut"), T.u[:, :])
     last = None
-    for c0, c1 in CH:
+    for c0, c1 in LD:
         last = load("y", view("t0", 4 * c0, 4 * c1), T.x[:, 4 * c0:4 * c1])
     load("y", view("w_q"), T.wc[:, :], code=True, after=[last], group="w")
     load("y", view("w_s"), T.ws[:, :], group="w")
 
-    def product_z(r, k):
-        mm(4 + k, "u_", 0, "a%d" % r, CH[k][0], CH[k][1])
+    def state(r, c0, c1, bank):
+        w0 = wide(c0, c1)
+        quant("a%d" % r, w0, c1, "t%d" % r, 4 * w0)
+        mm(bank, "u_", 0, "a%d" % r, w0, c1)
+        if r == WHOLE and c1 in CFG["pieces"]:
+            send(r, "a%d" % r, ([0] + CFG["pieces"])[CFG["pieces"].index(c1)], c1, "lw", "arw")
 
-    def signs(r, k):
-        c0, c1 = CH[k]
-        o = view("bt", c0, c1) if r < ROUNDS else view("bw", 4 * c0, 4 * c1, 4)
-        z = view("ps%d" % (4 + k), 0, c1 - c0)
-        if k == 2:
-            ts(o, z, 0.0, 2.0, ALU.is_gt, ALU.mult)
-        elif r < ROUNDS:
-            act(o, z, ACT.Sign, bias=-EPS, group="sg%d" % r)
-        else:
-            act(o, z, ACT.Sign, bias=-EPS)
+    def signs(r, c0, c1, bank):
+        w0 = wide(c0, c1)
+        o = view("bk", BT + c0, BT + c1) if r < ROUNDS else view("bw", 4 * c0, 4 * c1, 4)
+        act(o, view("ps%d" % bank, c0 - w0, c1 - w0), ACT.Sign, bias=-EPS)
 
-    def send(r, src, lo, hi):
+    def write(r, o, i, sem, code=False):
         dst = T.cores[rank ^ (1 << r)]
         rid, pid = topo.addr(dst)[0], topo.addr(dst)[1]
-        mask = topo.mask(core, dst)
-        vq, vs, lq, ls = view(src + "q", lo, hi), view(src + "s", lo, hi), view("l%dq" % r, lo, hi), view("l%ds" % r, lo, hi)
-        arr = T.sem["arr%d" % r]
-        op("g", lambda g: g.remote_dma(lq[0].bitcast(dt.uint8), vq[0].bitcast(dt.uint8), arr, T.sem.sent, pid, rid, mask),
-           [vq], [], sem="remote")
-        op("g", lambda g: g.remote_dma(ls[0], vs[0], arr, T.sem.sent, pid, rid, mask), [vs], [], sem="remote")
-        return 2 * len(topo.engines(core, dst))
+        to, src = (o[0].bitcast(dt.uint8), i[0].bitcast(dt.uint8)) if code else (o[0], i[0])
+        op("g", lambda g: g.remote_dma(to, src, T.sem[sem], T.sem.sent, pid, rid, topo.mask(core, dst)), [i], [], sem="remote")
+        count[sem] = count.get(sem, 0) + len(topo.engines(core, dst))
 
-    def clocks(r, head):
+    def send(r, src, lo, hi, land, sem):
+        write(r, view(land + "q", lo, hi), view(src + "q", lo, hi), sem, True)
+        write(r, view(land + "s", lo, hi), view(src + "s", lo, hi), sem)
+
+    def landed(sem, *views):
+        ops.append({"q": None, "fn": None, "r": [], "w": list(views), "group": None, "acc": False,
+                    "after": [], "sem": (sem, count[sem]), "dma": False})
+
+    def unpack(q, b):
+        o, i = view("da", b, 4 * CFG["da"], 4), view("ps%d" % b, 0, CFG["da"])
+        if q == "v":
+            vcopy(o, i)
+        else:
+            act(o, i, ACT.Copy)
+
+    def gtile(k):
+        o = view("gt", 512 * k, 512 * k + 512)
+        if k == G_C:
+            act(o, view("gt", 512 * G_F, 512 * G_F + 512), ACT.Identity, scale=-8.0)
+        else:
+            ts(o, view("sq"), (30.0, 4.0, 1.5625)[k], 0.5, ALU.is_equal if k == G_F else ALU.is_lt, ALU.mult)
+
+    def clocks(r):
         t, a = "t%d" % r, "a%d" % r
-
-        def per_step():
-            op("v", lambda g: g.vector.reciprocal(view("rs")[0], S[0]), [S], [view("rs")], group="px%d" % r)
-            tt(view("cx"), view("cq"), view("ps5", 0, NW), ALU.subtract, group="px%d" % r)
-
-        quant("b_", 0, 128, "bt", 0)
+        quant("b_", 0, 128, "bk", BT)
+        mm(B_TOT, "g_", 128 * G_TOT, "b_", 0, 128)
+        mm(B_REST, "g_", 128 * G_REST, "b_", 0, 128)
+        for b in range(0 if r == 0 else 4 if r == WHOLE else 2):
+            mm(b, "e_", 128 * b, a, 0, TC)
+        scan(view("cw", 0, NW), view("ps%d" % B_TOT, 0, NW), view("c36"), 0.0, ALU.add, ALU.add)
+        for c in range(8):
+            act(view("junk", NB * c, NB * c + NB), view("cw", 3, NW, 4), ACT.Sign, bias=S, scale=col("thc", c),
+                accum=col("acc", c), group="acc%d" % r)
+        tt(view("cq"), view("cw", 0, NW), view("ps%d" % B_REST, 0, NW), ALU.subtract)
+        scan(view("ee"), view("me"), view("cw", 3, 128, 4), 0.0, ALU.max, ALU.min)
+        if CFG["thr"] == "v":
+            ts(view("thr"), view("krow"), S, C_A, ALU.mult, ALU.add)
+        scan(view("cs"), view("mw"), view("cq"), 0.0, ALU.max, ALU.min)
         if r == 0:
-            quant("g_", 128, 384, "gt", 128)
-        mm(7, "g_", 128 * G_TOT, "b_", 0, 128)
-        mm(4, "g_", 128 * G_SUF, "b_", 0, 128)
-        mm(5, "g_", 128 * G_F, "b_", 0, 128)
-        if r > 0:
+            quant("g_", 256, 512, "gt", 1024)
+        else:
+            recip(view("rs"), S)
+        if CFG["thr"] == "s":
+            act(view("thr"), view("krow"), ACT.Identity, bias=C_A, scale=S)
+        for h in range(2):
+            act(view("bk", KT + 128 * h, KT + 128 * h + 128), view("nkrow"), ACT.Sign, bias=col("ee", 16 * h + 15), scale=S,
+                group="kb%d" % r)
+        if r == WHOLE:
+            unpack("s", 0)
+            unpack("s", 1)
+        ts(view("offb"), view("acc"), 2.0, float(2 * NB + 3), ALU.mult, ALU.add)
+        tt(view("bk", FT, FT + 128), view("cs"), view("thr"), ALU.is_le, off=view("offb"))
+        quant("k_", 0, 160, "bk", KT)
+        mm(B_F, "g_", 128 * G_C, "k_", 0, 128, True, False, group="f%d" % r)
+        mm(B_F, "g_", 128 * G_C, "k_", 32, 160, False, False, group="f%d" % r)
+        quant("f_", 0, 128, "bk", FT)
+        mm(B_F, "g_", 128 * G_F, "f_", 0, 128, False, True, group="f%d" % r)
+        if r == 0:
+            quant("e_", 0, 128, "et", 3)
+            quant("e_", 128, 256, "et", 2)
             mm(0, "e_", 0, a, 0, TC)
             mm(1, "e_", 128, a, 0, TC)
-        scan(view("cw", 0, NW), view("ps7", 0, NW), view("c36"), 0.0, ALU.add, ALU.add)
-        if r == 0:
-            memset(view("kt", 256, 640), 0.0)
-        act(view("thc"), view("kcol"), ACT.Identity, bias=1.0 / 256, scale=S)
-        for c in range(8):
-            act(view("junk", NB * c, NB * c + NB), view("cw", 3, NW, 4), ACT.Sign, bias=col("thc", c), scale=-1.0,
-                accum=col("acc", c), group="acc%d" % r)
-        if r > 0:
-            for b in range(2):
-                act(view("da", b, 4 * N0, 4), view("ps%d" % b, 0, N0), ACT.Copy, group="da%d" % r)
-        scan(view("ee"), view("me"), view("cw", 3, 128, 4), 0.0, ALU.max, ALU.min)
-        tt(view("cq"), view("cw", 0, NW), view("ps4", 0, NW), ALU.subtract)
-        ts(view("kt", 0, 128), view("krow"), S, col("ee", 15), ALU.mult, ALU.is_ge, group="kb%d" % r)
-        ts(view("cq", W2, NW), view("cq", W2, NW), col("cc", 4), None, ALU.add)
-        ts(view("kt", 128, 256), view("krow"), S, col("ee", 31), ALU.mult, ALU.is_ge, group="kb%d" % r)
-        scan(view("cs"), view("mw"), view("cq"), 0.0, ALU.max, ALU.min, group="fine%d" % r)
-        quant("k_", 0, 160, "kt", 0)
-        ts(view("thr"), view("krow"), S, col("cc", 0), ALU.mult, ALU.add, group="fine%d" % r)
-        if r == 0:
-            quant("g_", 384, 512, "gt", 384)
-            act(col("cc", 1), col("cf", 1), ACT.Identity, bias=36.0, scale=-9.0)
-            act(col("cc", 5), col("cf", 1), ACT.Identity, bias=28.0, scale=-9.0)
-            act(col("cc", 2), ECOL, ACT.Identity, bias=MAGIC, scale=-128.0)
-        mm(6, "g_", 128 * G_C, "k_", 0, 128, True, False, group="f%d" % r)
-        mm(6, "g_", 128 * G_C, "k_", 32, 160, False, False, group="f%d" % r)
-        ts(view("offb"), view("acc"), 2.0, float(2 * NB + 3), ALU.mult, ALU.add)
-        tt(view("ft", 0, 128), view("cs"), view("thr"), ALU.is_le, off=view("offb"))
-        quant("f_", 0, 128, "ft", 0)
-        mm(6, "g_", 128 * G_F, "f_", 0, 128, False, True, group="f%d" % r)
-        if r == 0:
-            quant("e_", 0, 256, "et", 0)
-        else:
-            per_step()
-        ts(view("offv"), view("ps6", 0, 32), 8.0, ECOL, ALU.mult, ALU.add)
+        elif r != WHOLE:
+            unpack("s", 0)
+            mm(2, "e_", 256, a, 0, TC)
+            mm(3, "e_", 384, a, 0, TC)
+        ts(view("offv"), view("ps%d" % B_F, 0, 32), 8.0, C_E, ALU.mult, ALU.add)
+        if r == WHOLE:
+            write(r, view("offw"), view("offv"), "arr%d" % r)
+            landed("arr%d" % r, view("offw"))
+            landed("arw", view("lwq"), view("lws"))
+            for b in range(4):
+                mm(4 + (b + 1) % 4, "e_", 128 * b, "lw", 0, TC)
+
+            def theirs(q, b):
+                o, i = view("dw", b, 4 * TC, 4), view("ps%d" % (4 + (b + 1) % 4), 0, TC)
+                return vcopy(o, i, group="dw") if q == "v" else act(o, i, ACT.Copy, group="dw")
+            unpack("s", 2)
+            unpack("s", 3)
+            theirs("s", 0)
+            theirs("s", 2)
+            ts(view("p1"), view("cq"), C_A, view("rs"), ALU.subtract, ALU.mult)
+            ts(view("p2"), view("p1"), 128.0, DELTA - 0.5, ALU.mult, ALU.add)
+            theirs("v", 1)
+            ts(view("p1"), view("p2"), MAGIC, MAGIC + E0 // 4, ALU.add, ALU.subtract)
+            theirs("v", 3)
+            ts(view("offp"), view("p1"), 4.0, C_E, ALU.mult, ALU.add)
+            return
         vcopy(view("vt", 0, 256), view(t), off=view("offv", 0, 16), group="v%d" % r)
         act(view("vt", 256, 512), view(t), ACT.Copy, off=view("offv", 16, 32), group="v%d" % r)
         quant("v%d" % r, 0, M, "vt", 0)
-        n_inc = head + send(r, "v%d" % r, 1 if head else 0, M)
-        ops.append({"q": None, "fn": None, "r": [], "w": [view("l%dq" % r), view("l%ds" % r)], "group": None, "acc": False,
-                    "after": [], "sem": ("arr%d" % r, n_inc), "dma": False})
+        send(r, "v%d" % r, 1 if r == 0 else 0, M, "l%d" % r, "arr%d" % r)
+        landed("arr%d" % r, view("l%dq" % r), view("l%ds" % r))
         if r == 0:
-            mm(0, "e_", 0, a, 0, TC)
-            mm(1, "e_", 128, a, 0, TC)
-            quant("e_", 256, 512, "et", 256)
-        mm(2, "e_", 256, a, 0, TC)
-        mm(3, "e_", 384, a, 0, TC)
-        if r == 0:
-            per_step()
-        for b in range(0 if r == 0 else 2, 4):
-            act(view("da", b, 4 * N0, 4), view("ps%d" % b, 0, N0), ACT.Copy, group="da%d" % r)
-        ts(view("p1", 0, W2), view("cx", 0, W2), col("cc", 1), view("rs"), ALU.subtract, ALU.mult, group="p1%d" % r)
-        ts(view("p1", W2, NW), view("cx", W2, NW), col("cc", 5), view("rs"), ALU.subtract, ALU.mult, group="p1%d" % r)
+            quant("e_", 256, 384, "et", 1)
+            quant("e_", 384, 512, "et", 0)
+            mm(2, "e_", 256, a, 0, TC)
+            mm(3, "e_", 384, a, 0, TC)
+            recip(view("rs"), S)
+            unpack("s", 0)
+        unpack("s", 1)
+        unpack("s", 2)
+        ts(view("p1"), view("cq"), C_A, view("rs"), ALU.subtract, ALU.mult)
         ts(view("p2"), view("p1"), 128.0, DELTA - 0.5, ALU.mult, ALU.add)
-        ts(view("offp"), view("p2"), MAGIC, col("cc", 2), ALU.add, ALU.subtract)
-        if r == 1:
-            memset(view("bw", 0, 2 * TC), 0.0)
-            memset(view("c9", 0, CH[2][0]), 9.0)
-            memset(view("c9", CH[2][0], TC), 1.0)
-        if r == 2:
-            memset(view("bw", 2 * TC, 4 * TC), 0.0)
-        return n_inc
-
-    def steps(k):
-        quant("bw_", CH[k][0], CH[k][1], "bw", CH[k][0])
-        mm(k, "g_", 128 * G_TOT, "bw_", CH[k][0], CH[k][1])
+        unpack("v", 3)
+        ts(view("offp"), view("p2"), MAGIC, C_MAGIC, ALU.add, ALU.subtract)
+        if r == max(q for q in range(ROUNDS) if q != WHOLE):
+            memset(view("c9"), 9.0)
+            memset(view("bw"), 0.0)
 
     def mix(r):
-        t, a = "t%d" % (r + 1), "a%d" % (r + 1)
-        for b in range(4):
+        t = "t%d" % (r + 1)
+        if r == WHOLE:
+            vcopy(view("dv", 0, 256), view("dw"), off=view("offw", 0, 16), group="dv%d" % r)
+            act(view("dv", 256, 512), view("dw"), ACT.Copy, off=view("offw", 16, 32), group="dv%d" % r)
+        for b in range(4 * (r != WHOLE)):
             mm(4 + b, "e_", 128 * b, "l%d" % r, 0, M)
-        for b in range(4):
+        for b in range(4 * (r != WHOLE)):
             o, i = view("dv", 128 * b, 128 * b + 128), view("ps%d" % (4 + b), 0, M)
             if b % 2 == 1:
                 vcopy(o, i, group="dv%d" % r)
             else:
                 act(o, i, ACT.Copy, group="dv%d" % r)
-        for c0, c1 in CH[1:]:
-            act(view("dg", 4 * c0, 4 * c1), view("dv"), ACT.Copy, off=view("offp", c0 // 4, c1 // 4))
-
-        def add(k, b):
-            c0, c1 = CH[k]
-            tt(view("ht", 4 * c0 + b, 4 * c1, 4), view("dg", 4 * c0 + b, 4 * c1, 4), view("ps%d" % b, c0, c1), ALU.add,
-               group="add%d_%d" % (r, k))
-
-        for k, (c0, c1) in enumerate(CH):
-            if k == 0:
+        a = "a%d" % (r + 1)
+        for kind, c0, c1, bank, arg in CFG["last" if r + 1 == ROUNDS else "mix"]:
+            w0 = wide(c0, c1)
+            p = view("ps%d" % bank, c0 - w0, c1 - w0)
+            if kind == "G":
+                act(view("dg", 4 * c0, 4 * c1), view("dv"), ACT.Copy, off=view("offp", c0 // 4, c1 // 4))
+            elif kind == "p":
+                for b in [int(c) for c in arg]:
+                    tt(view("ht", 4 * c0 + b, 4 * c1, 4), view("dg", 4 * c0 + b, 4 * c1, 4), view("ps%d" % b, c0, c1), ALU.add,
+                       group="add%d_%d" % (r, c0))
+            elif kind == "g":
                 tt(view("ht", 4 * c0, 4 * c1), view("dv"), view("da", 4 * c0, 4 * c1), ALU.add,
                    off=view("offp", c0 // 4, c1 // 4))
-            else:
-                for b in range(k - 1, 4):
-                    add(k, b)
-                if k == 1:
-                    add(2, 0)
-            quant("h_", c0, c1, "ht", c0)
-            base = 0 if k == 2 else 4
-            for i in range(4):
-                mm(base + i, "w_", 128 * i, "h_", c0, c1)
-            if k == 2:
-                quant(a, CH[0][0], CH[0][1], t, CH[0][0])
-                product_z(r + 1, 0)
-            for i in range(4):
-                o, p = view(t, 4 * c0 + i, 4 * c1, 4), view("ps%d" % (base + i), 0, c1 - c0)
-                if k == 2 and i < 3:
-                    ts(o, p, 0.03125, None, ALU.mult, group="ev%d" % r)
+            elif kind == "h":
+                quant("h_", w0, c1, "ht", 4 * w0)
+                for i in range(4):
+                    mm(bank + i, "w_", 128 * i, "h_", w0, c1)
+            elif kind == "e":
+                for i in range(4):
+                    o, p = view(t, 4 * c0 + i, 4 * c1, 4), view("ps%d" % (bank + i), c0 - w0, c1 - w0)
+                    grp = "ev%d_%d" % (r, c0) if CFG["grp"] else None
+                    if arg[i] == "v":
+                        ts(o, p, 0.03125, None, ALU.mult, group=grp)
+                    elif arg[i] == "s":
+                        act(o, p, ACT.Copy, scale=0.03125, group=grp)
+            elif kind == "a":
+                state(r + 1, c0, c1, bank)
+            elif kind == "s":
+                signs(r + 1, c0, c1, bank)
+            elif kind == "oc":
+                q = view(a + "q", c0, c1)
+                store(arg, T.oc[:, 4 * c0:4 * c1], q[0].bitcast(dt.uint8), q)
+            elif kind == "os":
+                for n in range(4):
+                    store(arg[n], T.osc[4 * n:4 * n + 4, c0:c1], T[a + "s"][32 * n:32 * n + 4, c0:c1], view(a + "s", c0, c1))
+            elif kind == "y":
+                if arg == "s":
+                    act(view("yt", c0, c1), p, ACT.Copy)
                 else:
-                    act(o, p, ACT.Copy, scale=0.03125)
-        signs(r + 1, 0)
-        if r + 1 == ROUNDS:
-            act(view("yt", 0, N0), view("ps4", 0, N0), ACT.Copy)
-        for k in (1, 2):
-            quant(a, CH[k][0], CH[k][1], t, CH[k][0])
-            product_z(r + 1, k)
-            if k == 2 and r + 1 == ROUNDS:
-                steps(0)
-            signs(r + 1, k)
+                    vcopy(view("yt", c0, c1), p)
+            elif kind == "oy":
+                store(arg, T.y[:, c0:c1], view("yt", c0, c1)[0], view("yt", c0, c1))
+            elif kind == "b":
+                quant("bw_", w0, c1, "bw", 4 * w0)
+                mm(bank, "g_", 128 * G_TOT, "bw_", w0, c1)
+            elif kind == "c":
+                scan(view("ct", c0, c1), p, view("c9", c0, c1), col("ct", c0 - 1) if c0 else 0.0, ALU.add, ALU.add)
+            elif kind == "cl":
+                store(arg, T.cl[:, c0:c1], T.ct[0:128:16, c0:c1], view("ct", c0, c1))
 
-    def outputs():
-        a = "a%d" % ROUNDS
-        q = view(a + "q", 0, N0)
-        store("y", T.oc[:, 0:4 * N0], q[0].bitcast(dt.uint8), q)
-        q = view(a + "q", N0, TC)
-        store("y", T.oc[:, 4 * N0:4 * TC], q[0].bitcast(dt.uint8), q)
-        store("y", T.y[:, 0:N0], view("yt", 0, N0)[0], view("yt", 0, N0))
-        for k in range(4):
-            store("y", T.osc[4 * k:4 * k + 4, 0:TC], T[a + "s"][32 * k:32 * k + 4, 0:TC], view(a + "s"))
-        for k in (1, 2):
-            c0, c1 = CH[k]
-            act(view("yt", c0, c1), view("ps%d" % (4 + k), 0, c1 - c0), ACT.Copy, group="y")
-        store("s", T.y[:, N0:TC], view("yt", N0, TC)[0], view("yt", N0, TC))
-        steps(1)
-        steps(2)
-        for k, (c0, c1) in enumerate(CH):
-            scan(view("ct", c0, c1), view("ps%d" % k, 0, c1 - c0), view("c9", c0, c1),
-                 col("ct", c0 - 1) if c0 else 0.0, ALU.add, ALU.add)
-        store("y", T.cl[:, :], T.ct[0:128:16, 0:TC], view("ct"))
-
-    def gtile(k):
-        for t in range(4):
-            o = view("gt", 512 * k + t, 512 * k + 512, 4)
-            ts(o, view("yy"), 16.0 if k == G_TOT else float(t * t), 0.5, ALU.is_equal if k == G_F else ALU.is_lt, ALU.mult,
-               group="gt%d" % k)
-
-    def etile(b):
-        o, h = view("et", 512 * b, 512 * b + 512), view("half")
-        op("g", lambda g: g.affine_select(o[0], h[0], [[-4, 128], [-1, 4]], ALU.is_equal, 0.0, b, 4), [h], [o])
-
-    def first(k):
-        quant("a0", CH[k][0], CH[k][1], "t0", CH[k][0])
-        product_z(0, k)
-
-    iota(view("pi"), [[0, 1]], 1)
-    iota(view("uu"), [[-8, 8], [-1, 4], [0, 4]])
+    iota(view("pf"), [[3072 - 768 - E0, 2]], 768 + E0, 1)
     iota(view("nrow"), [[1, 128]])
+    iota(view("uu"), [[-16, 8], [-1, 4], [0, 4]])
     iota(view("ie"), [[0, 2], [1, 16]])
-    iota(view("iw"), [[0, NB], [1, 4]])
-    memset(view("ft"), 0.0)
-    ts(col("ci", 0), view("pi"), 1, 0x38, ALU.logical_shift_right, ALU.bitwise_and, group="ci")
-    ts(col("ci", 1), view("pi"), 2, 3, ALU.logical_shift_right, ALU.bitwise_and, group="ci")
-    ts(col("ci", 2), view("pi"), 3, None, ALU.bitwise_and, group="ci")
-    ts(col("ci", 3), view("pi"), 15, None, ALU.bitwise_and, group="ci")
-    memset(view("bt", TC, 512), 0.0)
-    vcopy(view("cf"), view("ci"))
-    memset(view("half"), 0.5)
-    memset(view("c36", 0, W2), 36.0, group="c36")
-    memset(view("c36", W2, NW), 4.0, group="c36")
-    act(view("et", 1536, 2048), view("ft"), ACT.Identity)
-    act(view("yy"), view("uu"), ACT.Square, bias=col("cf", 0))
-    act(col("cc", 3), col("cf", 3), ACT.Identity, scale=1.0 / 128)
-    act(view("krow"), view("nrow"), ACT.Identity, scale=1.0 / 128)
-    act(view("kcol"), view("nrow", 0, 128, 16), ACT.Identity, bias=col("cc", 3), scale=1.0 / 128)
-    act(col("cc", 0), col("cf", 1), ACT.Identity, bias=27.0, scale=-9.0)
-    act(col("cc", 4), col("cf", 1), ACT.Identity, bias=24.0, scale=-8.0)
-    etile(0)
-    memset(view("cw", NW, 128), BIG)
-    ts(view("me"), view("ie"), col("cf", 3), BIG, ALU.is_equal, ALU.mult)
-    gtile(G_TOT)
-    quant("u_", 0, 128, "ut", 0)
-    quant("g_", 0, 128, "gt", 0)
-    first(0)
-    signs(0, 0)
-    head = send(0, "a0", 0, 1)
-    etile(1)
-    etile(2)
-    o3, h3 = view("et", 1539, 2048, 4), view("half", 0, 128)
-    op("g", lambda g: g.affine_select(o3[0], h3[0], [[-1, 128]], ALU.is_equal, 0.0, 0, 1), [h3], [o3])
-    gtile(G_SUF)
-    first(1)
-    signs(0, 1)
-    gtile(G_F)
-    first(2)
-    ts(view("mw"), view("iw"), ECOL, BIG, ALU.is_equal, ALU.mult)
-    signs(0, 2)
-    act(view("gt", 512 * G_C, 512 * G_C + 512), view("gt", 512 * G_F, 512 * G_F + 512), ACT.Identity, scale=16.0)
-    sent = 0
+    iota(view("iw"), [[0, NB], [1, 4]], E0)
+    iota(view("c36"), [[0, NW]], 36)
+    iota(view("cw", NW, 128), [[0, 128 - NW]], int(BIG))
+    act(col("gh", 0), col("pf", 1), ACT.Identity, bias=-7.5 / 16, scale=1.0 / 16)
+    act(col("gh", 1), col("pf", 1), ACT.Identity, bias=192 - 3073.5 / 4, scale=1.0 / 4)
+    act(C_G, col("gh", 0), ACT.Identity, bias=-3073.25, scale=16.0)
+    act(C_I, col("gh", 0), ACT.Identity, bias=col("pf", 1), scale=-16.0)
+    act(C_E, col("gh", 1), ACT.Identity, bias=col("pf", 0), scale=-4.0)
+    act(view("b4"), view("nrow", 0, 4), ACT.Identity, bias=C_G)
+    act(C_K, C_I, ACT.Identity, bias=-2.0 ** -34, scale=-WIDE / 128)
+    for n in range(4):
+        act(view("sq", n, 512, 4), view("uu"), ACT.Square, bias=col("b4", n), group="sq")
+    act(view("kcol"), view("nrow", 0, 128, 16), ACT.Identity, bias=C_K, scale=-WIDE / 128)
+    act(C_T, col("gh", 0), ACT.Identity, bias=36.0 - 27 * 192, scale=36.0)
+
+    def piece(k):
+        state(0, LD[k][0], LD[k][1], B_Z + k)
+        signs(0, LD[k][0], LD[k][1], B_Z + k)
+        if k == 0:
+            send(0, "a0", 0, 1, "l0", "arr0")
+            act(view("krow"), view("nrow"), ACT.Identity, scale=1.0 / 128)
+            act(C_A, col("gh", 1), ACT.Identity, bias=C_T, scale=-9.0)
+        if k == 1:
+            act(view("nkrow"), view("nrow"), ACT.Identity, scale=-WIDE / 128)
+            act(C_MAGIC, C_E, ACT.Identity, bias=MAGIC + 128 * E0, scale=-128.0)
+
+    def half():
+        o = view("et")
+        memset(o, 0.5)
+        op("g", lambda g: g.affine_select(o[0], o[0], [[-1, 516]], ALU.is_equal, 0.0, 3, 4), [o], [o])
+
+    start = {"hf": half, "bz": lambda: memset(view("bk", BT + TC, BT + 512), 0.0), "qu": lambda: quant("u_", 0, 128, "ut", 0),
+             "a0": lambda: piece(0), "a1": lambda: piece(1), "a2": lambda: piece(2), "a3": lambda: piece(3),
+             "me": lambda: ts(view("me"), view("ie"), C_I, BIG, ALU.is_equal, ALU.mult),
+             "mw": lambda: ts(view("mw"), view("iw"), C_E, BIG, ALU.is_equal, ALU.mult),
+             "gt": lambda: gtile(G_TOT), "gs": lambda: gtile(G_REST), "gf": lambda: (gtile(G_F), gtile(G_C)),
+             "q0": lambda: quant("g_", 0, 256, "gt", 0), "rc": lambda: recip(view("thc"), view("kcol"))}
+    for step in CFG["start"].split():
+        start[step]()
     for r in range(ROUNDS):
-        sent += clocks(r, head if r == 0 else 0)
+        clocks(r)
         mix(r)
-    outputs()
-    return ops, sent
+    return ops, sum(count.values())
 
 
 def _clash(x, y):

from concourse.mybir import dt, AluOpType as ALU, ActivationFunctionType as ACT

TC, M, ROUNDS = 448, 128, 3
NW = TC // 4
NB = TC // 16
BIG = 1.0e6
EPS = 2.0 ** -120
MAGIC = 1.5 * 2.0 ** 23
DELTA = 2.0 ** -14
WIDE = 1.0 + 2.0 ** -21
E0 = 1020
FT, KT, BT = 0, 128, 384
BF, F32, I32, U16, Q4, U8 = "bfloat16", "float32", "int32", "uint16", "float8_e4m3fn_x4", "uint8"

CFG = {
    "ld": [(0, 176), (176, 320), (320, 448)],
    "thr": "s",
    "grp": False,
    "whole": 2,
    "pieces": [160, 320, 448],
    "start": "hf bz qu a0 me mw gt gs a1 q0 a2 rc gf",
}


def schedule(c1, c2, order, last, ev="ssss ssss vvvs"):
    ch, ev = [(0, c1), (c1, c2), (c2, TC), (0, c2), (0, TC), (c1, TC)], ev.split()

    def calls(text):
        out = []
        for step in text.split():
            head, _, arg = step.partition(":")
            kind, k = head[:-1], int(head[-1])
            bank = {"h": (4, 4, 0), "e": (4, 4, 0), "b": (0, 1, 2, 0), "c": (0, 1, 2, 0)}.get(kind, (4, 5, 6, 4, 0, 0))[k]
            out.append((kind, ch[k][0], ch[k][1], bank, arg or (ev[k] if kind == "e" else "")))
        return out
    CFG.update(da=c1, mix=calls(order), last=calls(last))


schedule(160, 320, "G1 G2 g0 p1:0 h0 e0 p1:123 p2:0 h1 e1 p2:123 h2 a0 e2 s0 a1 a2 s1 s2",
         "G1 G2 g0 p1:0 h0 e0 p1:123 p2:0 h1 e1 p2:123 h2 a0 e2 s0 oc0:y y0:s oy0:y a1 a2 oc5:y os4:yyyy "
         "s1 s2 b0 b1 c0 b2 c1 c2 cl4:y y1:s y2:s oy5:s")

SCRATCH = {}


def _sb(name, n, dtype):
    SCRATCH[name] = ("sbuf", [128, n], dtype)


def _mx(name, n):
    _sb(name + "q", n, Q4)
    _sb(name + "s", n, U8)


for _r in range(ROUNDS + 1):
    _sb("t%d" % _r, 4 * TC, BF)
    _mx("a%d" % _r, TC)
for _r in range(ROUNDS):
    _mx("v%d" % _r, M)
    _mx("l%d" % _r, M)
for _n, _w, _d in [("ut", 512, BF), ("et", 516, BF), ("gt", 2048, BF), ("bk", BT + 512, BF), ("sq", 512, BF),
                   ("bw", 4 * TC, BF), ("vt", 512, BF), ("ht", 4 * TC, BF), ("da", 4 * TC, BF), ("dv", 512, BF),
                   ("dg", 4 * TC, BF), ("krow", 128, BF), ("nkrow", 128, F32), ("pf", 2, F32), ("gh", 2, BF),
                   ("cc", 8, F32), ("b4", 4, F32), ("uu", 128, F32), ("nrow", 128, F32), ("kcol", 8, F32),
                   ("ie", 32, F32), ("iw", NW, F32), ("me", 32, F32), ("mw", NW, F32), ("c36", NW, F32),
                   ("c9", TC, BF), ("cw", 128, F32), ("cq", NW, F32), ("cs", NW, F32), ("ee", 32, F32),
                   ("thr", 128, F32), ("thc", 8, F32), ("acc", 8, F32), ("junk", 8 * NB, BF), ("offb", 8, U16),
                   ("offv", 32, U16), ("offp", NW, U16), ("rs", 1, F32), ("p1", NW, F32),
                   ("p2", NW, F32), ("yt", TC, F32), ("ct", TC, F32), ("dw", 4 * TC, BF), ("offw", 32, U16)]:
    _sb(_n, _w, _d)
_mx("lw", TC)
for _n, _w in [("u", 128), ("w", 512), ("e", 512), ("g", 512), ("b", 128), ("f", 128), ("k", 160), ("h", TC), ("bw", TC)]:
    _mx(_n + "_", _w)
for _b in range(8):
    SCRATCH["ps%d" % _b] = ("psum", [128, 512], F32)

POOL = ["s%d" % _i for _i in range(140)]
SEMAPHORES = POOL + ["arr%d" % _r for _r in range(ROUNDS)] + ["arw", "sent", "out"]


def _plan(T, topo, core, rank):
    ops = []

    def view(name, lo=0, hi=None, step=1):
        hi = SCRATCH[name][1][1] if hi is None else hi
        bits = 0
        if step == 1:
            bits = ((1 << (hi - lo)) - 1) << lo
        else:
            for c in range(lo, hi, step):
                bits |= 1 << c
        ap = T[name][:, lo:hi] if step == 1 else T[name][:, lo:hi:step]
        return (ap, name, bits)

    def op(q, fn, reads, writes, group=None, acc=False, after=(), sem=None, dma=False):
        ops.append({"q": q, "fn": fn, "r": [v for v in reads if isinstance(v, tuple)], "w": list(writes),
                    "group": group, "acc": acc, "after": list(after), "sem": sem, "dma": dma})
        return len(ops) - 1

    def ap(v):
        return v[0] if isinstance(v, tuple) else v

    def memset(o, c, **k):
        return op("v", lambda g: g.vector.memset(o[0], c), [], [o], **k)

    def ts(o, i, s1, s2, o0, o1=None, **k):
        if o1 is None:
            return op("v", lambda g: g.vector.tensor_scalar(o[0], i[0], ap(s1), None, o0), [i, s1], [o], **k)
        return op("v", lambda g: g.vector.tensor_scalar(o[0], i[0], ap(s1), ap(s2), o0, o1), [i, s1, s2], [o], **k)

    def tt(o, a, b, alu, off=None, **k):
        return op("v", lambda g: g.vector.tensor_tensor(o[0], a[0] if off is None else a[0].indirect(off[0]), b[0], alu),
                  [a, b, off], [o], **k)

    def vcopy(o, i, off=None, **k):
        return op("v", lambda g: g.vector.tensor_copy(o[0], i[0] if off is None else i[0].indirect(off[0])),
                  [i, off], [o], **k)

    def scan(o, d0, d1, init, o0, o1, **k):
        return op("v", lambda g: g.vector.tensor_tensor_scan(o[0], d0[0], d1[0], ap(init), o0, o1), [d0, d1, init], [o], **k)

    def recip(o, i, **k):
        return op("v", lambda g: g.vector.reciprocal(o[0], i[0]), [i], [o], **k)

    def act(o, i, f, bias=0.0, scale=1.0, accum=None, off=None, **k):
        def fn(g):
            src = i[0] if off is None else i[0].indirect(off[0])
            if accum is None:
                return g.scalar.activation(o[0], src, f, bias=ap(bias), scale=ap(scale))
            return g.scalar.activation(o[0], src, f, bias=ap(bias), scale=ap(scale), accum_out=accum[0])
        return op("s", fn, [i, bias, scale, off], [o] + ([accum] if accum else []), **k)

    def quant(name, lo, hi, src, first, **k):
        q, s, i = view(name + "q", lo, hi), view(name + "s", lo, hi), view(src, first, first + 4 * (hi - lo))
        return op("v", lambda g: g.vector.quantize_mx(q[0], s[0], i[0]), [i], [q, s], **k)

    def mm(bank, lname, l0, rname, r0, r1, start=True, stop=True, **k):
        o = view("ps%d" % bank, 0, r1 - r0)
        lq, ls = view(lname + "q", l0, l0 + 128), view(lname + "s", l0, l0 + 128)
        rq, rsc = view(rname + "q", r0, r1), view(rname + "s", r0, r1)
        return op("t", lambda g: g.tensor.matmul_mx(o[0], lq[0], ls[0], rq[0], rsc[0], start, stop),
                  [lq, ls, rq, rsc], [o], acc=not start, **k)

    def iota(o, pattern, base=0, cm=0):
        return op("g", lambda g: g.iota(o[0], pattern, base, cm, allow_small_or_imprecise_dtypes=True), [], [o])

    def load(q, o, src, code=False, **k):
        dst = o[0].bitcast(dt.uint8) if code else o[0]
        if q == "y":
            return op("y", lambda g: g.sync.dma_start(dst, src), [], [o], dma=True, **k)
        return op("s", lambda g: g.scalar.dma_start(dst, src), [], [o], dma=True, **k)

    def store(q, dst, src, i):
        if q == "y":
            return op("y", lambda g: g.sync.dma_start(dst, src), [i], [], dma=True, sem="out")
        return op("s", lambda g: g.scalar.dma_start(dst, src), [i], [], dma=True, sem="out")

    G_TOT, G_REST, G_F, G_C = 0, 1, 2, 3
    B_Z, B_TOT, B_REST, B_F = 4, 6, 7, 4
    col = lambda name, c: view(name, c, c + 1)
    S = col("cw", NW - 1)
    C_E, C_I, C_A, C_MAGIC, C_G, C_K, C_T = [col("cc", c) for c in range(7)]
    LD, WHOLE, count = CFG["ld"], CFG["whole"], {}
    wide = lambda c0, c1: min(c0, c1 - 128)

    load("s", view("ut"), T.u[:, :])
    last = None
    for c0, c1 in LD:
        last = load("y", view("t0", 4 * c0, 4 * c1), T.x[:, 4 * c0:4 * c1])
    load("y", view("w_q"), T.wc[:, :], code=True, after=[last], group="w")
    load("y", view("w_s"), T.ws[:, :], group="w")

    def state(r, c0, c1, bank):
        w0 = wide(c0, c1)
        quant("a%d" % r, w0, c1, "t%d" % r, 4 * w0)
        mm(bank, "u_", 0, "a%d" % r, w0, c1)
        if r == WHOLE and c1 in CFG["pieces"]:
            send(r, "a%d" % r, ([0] + CFG["pieces"])[CFG["pieces"].index(c1)], c1, "lw", "arw")

    def signs(r, c0, c1, bank):
        w0 = wide(c0, c1)
        o = view("bk", BT + c0, BT + c1) if r < ROUNDS else view("bw", 4 * c0, 4 * c1, 4)
        act(o, view("ps%d" % bank, c0 - w0, c1 - w0), ACT.Sign, bias=-EPS)

    def write(r, o, i, sem, code=False):
        dst = T.cores[rank ^ (1 << r)]
        rid, pid = topo.addr(dst)[0], topo.addr(dst)[1]
        to, src = (o[0].bitcast(dt.uint8), i[0].bitcast(dt.uint8)) if code else (o[0], i[0])
        op("g", lambda g: g.remote_dma(to, src, T.sem[sem], T.sem.sent, pid, rid, topo.mask(core, dst)), [i], [], sem="remote")
        count[sem] = count.get(sem, 0) + len(topo.engines(core, dst))

    def send(r, src, lo, hi, land, sem):
        write(r, view(land + "q", lo, hi), view(src + "q", lo, hi), sem, True)
        write(r, view(land + "s", lo, hi), view(src + "s", lo, hi), sem)

    def landed(sem, *views):
        ops.append({"q": None, "fn": None, "r": [], "w": list(views), "group": None, "acc": False,
                    "after": [], "sem": (sem, count[sem]), "dma": False})

    def unpack(q, b):
        o, i = view("da", b, 4 * CFG["da"], 4), view("ps%d" % b, 0, CFG["da"])
        if q == "v":
            vcopy(o, i)
        else:
            act(o, i, ACT.Copy)

    def gtile(k):
        o = view("gt", 512 * k, 512 * k + 512)
        if k == G_C:
            act(o, view("gt", 512 * G_F, 512 * G_F + 512), ACT.Identity, scale=-8.0)
        else:
            ts(o, view("sq"), (30.0, 4.0, 1.5625)[k], 0.5, ALU.is_equal if k == G_F else ALU.is_lt, ALU.mult)

    def clocks(r):
        t, a = "t%d" % r, "a%d" % r
        quant("b_", 0, 128, "bk", BT)
        mm(B_TOT, "g_", 128 * G_TOT, "b_", 0, 128)
        mm(B_REST, "g_", 128 * G_REST, "b_", 0, 128)
        for b in range(0 if r == 0 else 4 if r == WHOLE else 2):
            mm(b, "e_", 128 * b, a, 0, TC)
        scan(view("cw", 0, NW), view("ps%d" % B_TOT, 0, NW), view("c36"), 0.0, ALU.add, ALU.add)
        for c in range(8):
            act(view("junk", NB * c, NB * c + NB), view("cw", 3, NW, 4), ACT.Sign, bias=S, scale=col("thc", c),
                accum=col("acc", c), group="acc%d" % r)
        tt(view("cq"), view("cw", 0, NW), view("ps%d" % B_REST, 0, NW), ALU.subtract)
        scan(view("ee"), view("me"), view("cw", 3, 128, 4), 0.0, ALU.max, ALU.min)
        if CFG["thr"] == "v":
            ts(view("thr"), view("krow"), S, C_A, ALU.mult, ALU.add)
        scan(view("cs"), view("mw"), view("cq"), 0.0, ALU.max, ALU.min)
        if r == 0:
            quant("g_", 256, 512, "gt", 1024)
        else:
            recip(view("rs"), S)
        if CFG["thr"] == "s":
            act(view("thr"), view("krow"), ACT.Identity, bias=C_A, scale=S)
        for h in range(2):
            act(view("bk", KT + 128 * h, KT + 128 * h + 128), view("nkrow"), ACT.Sign, bias=col("ee", 16 * h + 15), scale=S,
                group="kb%d" % r)
        if r == WHOLE:
            unpack("s", 0)
            unpack("s", 1)
        ts(view("offb"), view("acc"), 2.0, float(2 * NB + 3), ALU.mult, ALU.add)
        tt(view("bk", FT, FT + 128), view("cs"), view("thr"), ALU.is_le, off=view("offb"))
        quant("k_", 0, 160, "bk", KT)
        mm(B_F, "g_", 128 * G_C, "k_", 0, 128, True, False, group="f%d" % r)
        mm(B_F, "g_", 128 * G_C, "k_", 32, 160, False, False, group="f%d" % r)
        quant("f_", 0, 128, "bk", FT)
        mm(B_F, "g_", 128 * G_F, "f_", 0, 128, False, True, group="f%d" % r)
        if r == 0:
            quant("e_", 0, 128, "et", 3)
            quant("e_", 128, 256, "et", 2)
            mm(0, "e_", 0, a, 0, TC)
            mm(1, "e_", 128, a, 0, TC)
        elif r != WHOLE:
            unpack("s", 0)
            mm(2, "e_", 256, a, 0, TC)
            mm(3, "e_", 384, a, 0, TC)
        ts(view("offv"), view("ps%d" % B_F, 0, 32), 8.0, C_E, ALU.mult, ALU.add)
        if r == WHOLE:
            write(r, view("offw"), view("offv"), "arr%d" % r)
            landed("arr%d" % r, view("offw"))
            landed("arw", view("lwq"), view("lws"))
            for b in range(4):
                mm(4 + (b + 1) % 4, "e_", 128 * b, "lw", 0, TC)

            def theirs(q, b):
                o, i = view("dw", b, 4 * TC, 4), view("ps%d" % (4 + (b + 1) % 4), 0, TC)
                return vcopy(o, i, group="dw") if q == "v" else act(o, i, ACT.Copy, group="dw")
            unpack("s", 2)
            unpack("s", 3)
            theirs("s", 0)
            theirs("s", 2)
            ts(view("p1"), view("cq"), C_A, view("rs"), ALU.subtract, ALU.mult)
            ts(view("p2"), view("p1"), 128.0, DELTA - 0.5, ALU.mult, ALU.add)
            theirs("v", 1)
            ts(view("p1"), view("p2"), MAGIC, MAGIC + E0 // 4, ALU.add, ALU.subtract)
            theirs("v", 3)
            ts(view("offp"), view("p1"), 4.0, C_E, ALU.mult, ALU.add)
            return
        vcopy(view("vt", 0, 256), view(t), off=view("offv", 0, 16), group="v%d" % r)
        act(view("vt", 256, 512), view(t), ACT.Copy, off=view("offv", 16, 32), group="v%d" % r)
        quant("v%d" % r, 0, M, "vt", 0)
        send(r, "v%d" % r, 1 if r == 0 else 0, M, "l%d" % r, "arr%d" % r)
        landed("arr%d" % r, view("l%dq" % r), view("l%ds" % r))
        if r == 0:
            quant("e_", 256, 384, "et", 1)
            quant("e_", 384, 512, "et", 0)
            mm(2, "e_", 256, a, 0, TC)
            mm(3, "e_", 384, a, 0, TC)
            recip(view("rs"), S)
            unpack("s", 0)
        unpack("s", 1)
        unpack("s", 2)
        ts(view("p1"), view("cq"), C_A, view("rs"), ALU.subtract, ALU.mult)
        ts(view("p2"), view("p1"), 128.0, DELTA - 0.5, ALU.mult, ALU.add)
        unpack("v", 3)
        ts(view("offp"), view("p2"), MAGIC, C_MAGIC, ALU.add, ALU.subtract)
        if r == max(q for q in range(ROUNDS) if q != WHOLE):
            memset(view("c9"), 9.0)
            memset(view("bw"), 0.0)

    def mix(r):
        t = "t%d" % (r + 1)
        if r == WHOLE:
            vcopy(view("dv", 0, 256), view("dw"), off=view("offw", 0, 16), group="dv%d" % r)
            act(view("dv", 256, 512), view("dw"), ACT.Copy, off=view("offw", 16, 32), group="dv%d" % r)
        for b in range(4 * (r != WHOLE)):
            mm(4 + b, "e_", 128 * b, "l%d" % r, 0, M)
        for b in range(4 * (r != WHOLE)):
            o, i = view("dv", 128 * b, 128 * b + 128), view("ps%d" % (4 + b), 0, M)
            if b % 2 == 1:
                vcopy(o, i, group="dv%d" % r)
            else:
                act(o, i, ACT.Copy, group="dv%d" % r)
        a = "a%d" % (r + 1)
        for kind, c0, c1, bank, arg in CFG["last" if r + 1 == ROUNDS else "mix"]:
            w0 = wide(c0, c1)
            p = view("ps%d" % bank, c0 - w0, c1 - w0)
            if kind == "G":
                act(view("dg", 4 * c0, 4 * c1), view("dv"), ACT.Copy, off=view("offp", c0 // 4, c1 // 4))
            elif kind == "p":
                for b in [int(c) for c in arg]:
                    tt(view("ht", 4 * c0 + b, 4 * c1, 4), view("dg", 4 * c0 + b, 4 * c1, 4), view("ps%d" % b, c0, c1), ALU.add,
                       group="add%d_%d" % (r, c0))
            elif kind == "g":
                tt(view("ht", 4 * c0, 4 * c1), view("dv"), view("da", 4 * c0, 4 * c1), ALU.add,
                   off=view("offp", c0 // 4, c1 // 4))
            elif kind == "h":
                quant("h_", w0, c1, "ht", 4 * w0)
                for i in range(4):
                    mm(bank + i, "w_", 128 * i, "h_", w0, c1)
            elif kind == "e":
                for i in range(4):
                    o, p = view(t, 4 * c0 + i, 4 * c1, 4), view("ps%d" % (bank + i), c0 - w0, c1 - w0)
                    grp = "ev%d_%d" % (r, c0) if CFG["grp"] else None
                    if arg[i] == "v":
                        ts(o, p, 0.03125, None, ALU.mult, group=grp)
                    elif arg[i] == "s":
                        act(o, p, ACT.Copy, scale=0.03125, group=grp)
            elif kind == "a":
                state(r + 1, c0, c1, bank)
            elif kind == "s":
                signs(r + 1, c0, c1, bank)
            elif kind == "oc":
                q = view(a + "q", c0, c1)
                store(arg, T.oc[:, 4 * c0:4 * c1], q[0].bitcast(dt.uint8), q)
            elif kind == "os":
                for n in range(4):
                    store(arg[n], T.osc[4 * n:4 * n + 4, c0:c1], T[a + "s"][32 * n:32 * n + 4, c0:c1], view(a + "s", c0, c1))
            elif kind == "y":
                if arg == "s":
                    act(view("yt", c0, c1), p, ACT.Copy)
                else:
                    vcopy(view("yt", c0, c1), p)
            elif kind == "oy":
                store(arg, T.y[:, c0:c1], view("yt", c0, c1)[0], view("yt", c0, c1))
            elif kind == "b":
                quant("bw_", w0, c1, "bw", 4 * w0)
                mm(bank, "g_", 128 * G_TOT, "bw_", w0, c1)
            elif kind == "c":
                scan(view("ct", c0, c1), p, view("c9", c0, c1), col("ct", c0 - 1) if c0 else 0.0, ALU.add, ALU.add)
            elif kind == "cl":
                store(arg, T.cl[:, c0:c1], T.ct[0:128:16, c0:c1], view("ct", c0, c1))

    iota(view("pf"), [[3072 - 768 - E0, 2]], 768 + E0, 1)
    iota(view("nrow"), [[1, 128]])
    iota(view("uu"), [[-16, 8], [-1, 4], [0, 4]])
    iota(view("ie"), [[0, 2], [1, 16]])
    iota(view("iw"), [[0, NB], [1, 4]], E0)
    iota(view("c36"), [[0, NW]], 36)
    iota(view("cw", NW, 128), [[0, 128 - NW]], int(BIG))
    act(col("gh", 0), col("pf", 1), ACT.Identity, bias=-7.5 / 16, scale=1.0 / 16)
    act(col("gh", 1), col("pf", 1), ACT.Identity, bias=192 - 3073.5 / 4, scale=1.0 / 4)
    act(C_G, col("gh", 0), ACT.Identity, bias=-3073.25, scale=16.0)
    act(C_I, col("gh", 0), ACT.Identity, bias=col("pf", 1), scale=-16.0)
    act(C_E, col("gh", 1), ACT.Identity, bias=col("pf", 0), scale=-4.0)
    act(view("b4"), view("nrow", 0, 4), ACT.Identity, bias=C_G)
    act(C_K, C_I, ACT.Identity, bias=-2.0 ** -34, scale=-WIDE / 128)
    for n in range(4):
        act(view("sq", n, 512, 4), view("uu"), ACT.Square, bias=col("b4", n), group="sq")
    act(view("kcol"), view("nrow", 0, 128, 16), ACT.Identity, bias=C_K, scale=-WIDE / 128)
    act(C_T, col("gh", 0), ACT.Identity, bias=36.0 - 27 * 192, scale=36.0)

    def piece(k):
        state(0, LD[k][0], LD[k][1], B_Z + k)
        signs(0, LD[k][0], LD[k][1], B_Z + k)
        if k == 0:
            send(0, "a0", 0, 1, "l0", "arr0")
            act(view("krow"), view("nrow"), ACT.Identity, scale=1.0 / 128)
            act(C_A, col("gh", 1), ACT.Identity, bias=C_T, scale=-9.0)
        if k == 1:
            act(view("nkrow"), view("nrow"), ACT.Identity, scale=-WIDE / 128)
            act(C_MAGIC, C_E, ACT.Identity, bias=MAGIC + 128 * E0, scale=-128.0)

    def half():
        o = view("et")
        memset(o, 0.5)
        op("g", lambda g: g.affine_select(o[0], o[0], [[-1, 516]], ALU.is_equal, 0.0, 3, 4), [o], [o])

    start = {"hf": half, "bz": lambda: memset(view("bk", BT + TC, BT + 512), 0.0), "qu": lambda: quant("u_", 0, 128, "ut", 0),
             "a0": lambda: piece(0), "a1": lambda: piece(1), "a2": lambda: piece(2), "a3": lambda: piece(3),
             "me": lambda: ts(view("me"), view("ie"), C_I, BIG, ALU.is_equal, ALU.mult),
             "mw": lambda: ts(view("mw"), view("iw"), C_E, BIG, ALU.is_equal, ALU.mult),
             "gt": lambda: gtile(G_TOT), "gs": lambda: gtile(G_REST), "gf": lambda: (gtile(G_F), gtile(G_C)),
             "q0": lambda: quant("g_", 0, 256, "gt", 0), "rc": lambda: recip(view("thc"), view("kcol"))}
    for step in CFG["start"].split():
        start[step]()
    for r in range(ROUNDS):
        clocks(r)
        mix(r)
    return ops, sum(count.values())


def _clash(x, y):
    for xs, ys, both_read in ((x["w"], y["r"], False), (x["w"], y["w"], False), (x["r"], y["w"], False), (x["r"], y["r"], True)):
        for a in xs:
            for b in ys:
                if a[1] != b[1]:
                    continue
                if a[1].startswith("ps"):
                    if x["q"] != y["q"] or not (both_read or y["acc"]):
                        return True
                elif not both_read and a[2] & b[2]:
                    return True
    return False


def _emit(g, T, ops, sent):
    members = {}
    for n, o in enumerate(ops):
        o["tok"] = o["group"] or ("#%d" % n)
        members.setdefault(o["tok"], []).append(n)
    known = {q: set() for q in "gvsty"}
    waited = []
    for n, o in enumerate(ops):
        o["waits"] = []
        if o["q"] is None:
            o["snap"] = set()
            continue
        k = known[o["q"]]
        for m in range(n - 1, -1, -1):
            if m in k or not (m in o["after"] or _clash(ops[m], o)):
                continue
            tok = ops[m]["tok"]
            assert tok != o["tok"] and members[tok][-1] < n, (tok, n)
            o["waits"].append(tok)
            if tok not in waited:
                waited.append(tok)
            for j in members[tok]:
                k.add(j)
                k |= ops[j]["snap"]
        o["snap"] = set(k)
    sem_of, state, fresh = {}, {}, list(POOL)
    for tok in sorted(waited, key=lambda t: members[t][0]):
        mem = members[tok]
        first = ops[mem[0]]
        if first["q"] is None:
            sem_of[tok] = first["sem"]
            continue
        assert first["sem"] is None
        inc = sum(16 if ops[j]["dma"] else 1 for j in mem)
        if fresh:
            name = fresh.pop(0)
            state[name] = [0, []]
        else:
            name = [s for s in POOL if all(p in ops[j]["snap"] for p in state[s][1] for j in mem)][0]
        state[name] = [state[name][0] + inc, mem]
        sem_of[tok] = (name, state[name][0])
    queue = {"g": g, "v": g.vector, "s": g.scalar, "t": g.tensor, "y": g.sync}
    outs = 0
    for o in ops:
        if o["q"] is None:
            continue
        for tok in o["waits"]:
            queue[o["q"]].wait_ge(T.sem[sem_of[tok][0]], sem_of[tok][1])
        ins = o["fn"](g)
        if o["sem"] == "out":
            ins.then_inc(T.sem.out, 16)
            outs += 16
        elif o["tok"] in sem_of:
            ins.then_inc(T.sem[sem_of[o["tok"]][0]], 16 if o["dma"] else 1)
    g.wait_ge(T.sem.sent, sent)
    g.sync.wait_ge(T.sem.out, outs)


def rank_program(g, core, T, topo):
    rank = T.rank_of(core)
    if rank is None:
        return
    ops, sent = _plan(T, topo, core, rank)
    _emit(g, T, ops, sent)
